import numpy as np
import ml_dtypes


def mxq(x, axis, fmt="e4m3"):
    dtype, down = {"e4m3": (ml_dtypes.float8_e4m3fn, 7), "e5m2": (ml_dtypes.float8_e5m2, 14)}[fmt]
    v = np.moveaxis(np.asarray(x, np.float32).astype(ml_dtypes.bfloat16).astype(np.float64), axis, -1)
    blocks = v.reshape(v.shape[:-1] + (-1, 32))
    amax = np.abs(blocks).max(-1, keepdims=True)
    byte = np.maximum(np.where(amax > 0, np.frexp(amax)[1] - 1 + 127, 0) - down, 1)
    scale = np.exp2(byte - 127.0)
    codes = (blocks / scale).astype(np.float32).astype(dtype).astype(np.float64)
    return np.moveaxis((codes * scale).reshape(v.shape), -1, axis)


WIDE = False


def mx_kscale(k):
    if not WIDE:
        return np.ones(k)
    levels = np.array([10, -10, 5, -5, 0])
    if k % 512:
        return np.exp2(np.random.permutation(np.resize(levels, k // 32))).repeat(32)
    a = np.empty((k // 512, 16))
    for p in range(k // 512):
        a[p, :8] = np.random.permutation(np.resize(levels, 8))
        for g in range(8):
            far = levels[np.abs(levels - a[p, g]) >= 10]
            a[p, g + 8] = far[np.random.randint(len(far))]
    return np.exp2(a.ravel()).repeat(32)


BF16 = ml_dtypes.bfloat16


def bf(x):
    return np.asarray(x, np.float32).astype(BF16)


def f64(x):
    return np.asarray(x).astype(np.float64)

def planes(Y):
    n, m = Y.shape
    b = f64(bf(Y)).reshape(n // 32, 32, m)
    amax = np.abs(b).max(1)
    byte = np.clip(np.where(amax > 0, np.frexp(amax)[1] - 1 + 127 - 7, 1), 1, 254)
    codes = (b * np.exp2(127.0 - byte)[:, None, :]).reshape(n, m).astype(np.float32).astype(ml_dtypes.float8_e4m3fn).view(np.uint8)
    words = codes.reshape(n // 512, 128, 4, m).transpose(0, 1, 3, 2)
    return np.ascontiguousarray(words), np.ascontiguousarray(byte.astype(np.uint8).reshape(n // 512, 16, m))


N, D, F = 1024, 2048, 1024
H = F // 2


def max_min(h):
    hl = h[:, :H]
    hr = h[:, H:]
    return np.concatenate([np.maximum(hl, hr), np.minimum(hl, hr)], axis=1)


def setup_inputs():
    a, u = mx_kscale(D), mx_kscale(F)
    return {
        "x": bf(np.random.standard_normal((N, D)) * a[None, :]),
        "w": bf(np.random.standard_normal((D, F)) / np.sqrt(D) / a[:, None]),
        "d": bf((1.0 + 0.2 * np.random.standard_normal(D)) * a * a),
        "s": bf((1.0 + 0.1 * np.random.standard_normal(F)) * u),
        "t": bf((1.0 + 0.1 * np.random.standard_normal(F)) / u),
        "b": bf(0.4 * np.random.standard_normal(F)),
    }


def core(x, w, d, s, t, b):
    x, w, d, s, t, b = f64(x), f64(w), f64(d), f64(s), f64(t), f64(b)
    wq = mxq(w, 0, "e4m3")
    p = mxq(x, 1, "e4m3") @ wq
    wd = d[:, None] * w
    g = mxq(wd, 0, "e4m3").T @ wq
    ps = p * s[None, :]
    gt = g * t[:, None]
    r = mxq(ps, 1, "e4m3") @ mxq(gt, 0, "e4m3")
    h = 1.5 * p - 0.5 * r + b[None, :]
    return max_min(h)


def reference(x, w, d, s, t, b):
    R_out = core(x, w, d, s, t, b)
    words, scales = planes(R_out)
    return R_out, words, scales

@@ -1,0 +1,717 @@
+from contextlib import ExitStack
+
+import concourse.mybir as mybir
+from concourse.masks import make_identity
+
+N, D, F = 1024, 2048, 1024
+FLOPS = 2 * N * F * (D + D + F)
+
+F32 = mybir.dt.float32
+BF16 = mybir.dt.bfloat16
+U32 = mybir.dt.uint32
+I32 = mybir.dt.int32
+U8 = mybir.dt.uint8
+FP8X4 = mybir.dt.float8_e4m3fn_x4
+ALU = mybir.AluOpType
+ACT = mybir.ActivationFunctionType
+
+P = 128
+W = 512
+NC = D // W
+T4_BUFS = 15
+H0T_BUFS = 14
+
+
+def tile_bjorckmaxmindense_x1_kernel(tc, x, w, d, s, t, b, out, out_words, out_scales):
+    nc = tc.nc
+    with ExitStack() as ctx:
+        const = ctx.enter_context(tc.tile_pool(name="const", bufs=1))
+        t8 = ctx.enter_context(tc.tile_pool(name="t8", bufs=4))
+        t4 = ctx.enter_context(tc.tile_pool(name="t4", bufs=T4_BUFS))
+        keep = ctx.enter_context(tc.tile_pool(name="keep", bufs=1))
+        h0tp = ctx.enter_context(tc.tile_pool(name="h0tp", bufs=H0T_BUFS))
+        h0p = ctx.enter_context(tc.tile_pool(name="h0p", bufs=5))
+        hp = ctx.enter_context(tc.tile_pool(name="hp", bufs=4))
+        oqp = ctx.enter_context(tc.tile_pool(name="oqp", bufs=2))
+        ps = ctx.enter_context(tc.psum_pool(name="ps", bufs=8))
+
+        d_cols = const.tile([P, NC, 4], BF16)
+        nc.scalar.dma_start(out=d_cols[:], in_=d.rearrange("(c p j) -> p c j", p=P, j=4))
+        s_bf = const.tile([P, 2, 4], BF16)
+        t_bf = const.tile([P, 2, 4], BF16)
+        b_bf = const.tile([P, 2, 4], BF16)
+        for tile_, vec in ((s_bf, s), (b_bf, b), (t_bf, t)):
+            nc.scalar.dma_start(out=tile_[:], in_=vec.rearrange("(g p t) -> p g t", p=P, t=4))
+        ident = const.tile([P, P], F32)
+        make_identity(nc, ident[:])
+
+        w_raw, x_raw = {}, {}
+
+        def load_w(g, c):
+            w_raw[g, c] = t4.tile([P, 4, W], BF16, name="t4", align_bytes=64)
+            src = w[c * W : (c + 1) * W, g * W : (g + 1) * W].rearrange("(p j) f -> p j f", j=4)
+            nc.sync.dma_start(out=w_raw[g, c][:], in_=src)
+
+        def load_x(tg, kh):
+            x_raw[tg, kh] = t8.tile([P, 4, 1024], BF16, name="t8", align_bytes=64)
+            src = x[tg * W : (tg + 1) * W, kh * 1024 : (kh + 1) * 1024].rearrange("(m t) k -> m t k", t=4)
+            nc.sync.dma_start(out=x_raw[tg, kh][:], in_=src)
+
+        load_w(0, 0)
+        load_w(0, 1)
+        load_x(0, 0)
+        load_w(0, 2)
+        load_w(0, 3)
+        load_x(0, 1)
+        for c in range(NC):
+            load_w(1, c)
+        load_x(1, 0)
+        load_x(1, 1)
+
+        s_cols = const.tile([P, 2, 4], F32)
+        nc.vector.tensor_copy(out=s_cols[:], in_=s_bf[:])
+        t_cols = const.tile([P, 2, 4], F32)
+        nc.vector.tensor_copy(out=t_cols[:], in_=t_bf[:])
+        b_cols = const.tile([P, 2, 4], F32)
+        nc.vector.tensor_copy(out=b_cols[:], in_=b_bf[:])
+
+        def codes(name, width):
+            return (
+                keep.tile([P, width], U32, name=name + "_q", align_bytes=64),
+                keep.tile([P, width], U8, name=name + "_s", align_bytes=64),
+            )
+
+        def quantize(dst, lo, width, src):
+            nc.vector.quantize_mx(
+                out=dst[0][:, lo : lo + width].bitcast(FP8X4),
+                scales=dst[1][:, lo : lo + width],
+                in_=src,
+            )
+
+        def mx(acc, lhs, l0, rhs, r0, n, start, stop):
+            nc.tensor.matmul_mx(
+                out=acc,
+                lhsT=lhs[0][:, l0 : l0 + P].bitcast(FP8X4),
+                lhsT_scale=lhs[1][:, l0 : l0 + P],
+                rhs=rhs[0][:, r0 : r0 + n].bitcast(FP8X4),
+                rhs_scale=rhs[1][:, r0 : r0 + n],
+                start=start,
+                stop=stop,
+            )
+
+        wq = {(g, c): codes("w%d%d" % (g, c), W) for g in range(2) for c in range(NC)}
+        wdq = {(g, c): codes("wd%d%d" % (g, c), W) for g in range(2) for c in range(NC)}
+        xq = {(tg, c): codes("x%d%d" % (tg, c), W) for tg in range(2) for c in range(NC)}
+        gq = {(gi, jg): codes("g%d%d" % (gi, jg), W) for gi in range(2) for jg in range(2)}
+        psq = {(tg, gi): codes("ps%d%d" % (tg, gi), W) for tg in range(2) for gi in range(2)}
+        wg, wdg = {}, {}
+
+        def w_group(g, c, on_scalar):
+            wg[g, c] = t4.tile([P, 4 * W], BF16, name="t4", align_bytes=64)
+            dst = wg[g, c][:].rearrange("p (t m j) -> p t m j", t=4, j=4)
+            src = w_raw[g, c][:].rearrange("p j (m t) -> p t m j", t=4)
+            if on_scalar:
+                nc.scalar.copy(out=dst, in_=src)
+            else:
+                nc.vector.tensor_copy(out=dst, in_=src)
+
+        def w_quant(g, c):
+            quantize(wq[g, c], 0, W, wg[g, c][:])
+
+        def wd_make(g, c):
+            wdg[g, c] = t4.tile([P, 4 * W], BF16, name="t4", align_bytes=64)
+            nc.vector.tensor_tensor(
+                out=wdg[g, c][:].rearrange("p (f j) -> p f j", j=4),
+                in0=wg[g, c][:].rearrange("p (f j) -> p f j", j=4),
+                in1=d_cols[:, c, :].unsqueeze(1).to_broadcast([P, W, 4]),
+                op=ALU.mult,
+            )
+
+        def wd_quant(g, c):
+            quantize(wdq[g, c], 0, W, wdg[g, c][:])
+
+        xg, xbank = {}, {}
+
+        def x_turn(tg, c, half):
+            words = x_raw[tg, c // 2][:].bitcast(F32)
+            k0 = 256 * (c % 2)
+            bank = ps.tile([P, 2, 2, P], F32, name="bank")
+            xbank[tg, c, half] = bank
+            for i in range(2):
+                for u in range(2):
+                    nc.tensor.transpose(bank[:, i, u, :], words[:, 2 * half + i, k0 + u : k0 + 256 : 2], ident[:])
+
+        def x_out(tg, c, half, on_vector=False):
+            if (tg, c) not in xg:
+                xg[tg, c] = t4.tile([P, W, 2], F32, name="t4", align_bytes=64)
+            dst = xg[tg, c][:, half * 256 : (half + 1) * 256, :].rearrange("p (i r) u -> p i r u", i=2)
+            src = xbank[tg, c, half][:].rearrange("p i u r -> p i r u")
+            if on_vector:
+                nc.vector.tensor_copy(out=dst, in_=src)
+            else:
+                nc.scalar.copy(out=dst, in_=src)
+
+        def x_quant(tg, c):
+            quantize(xq[tg, c], 0, W, xg[tg, c][:].rearrange("p r u -> p (r u)").bitcast(BF16))
+
+        h0t = {}
+        psraw = {}
+
+        def p_pass(acc, tg, slot, c):
+            mx(acc[:], wq[slot // 4, c], slot % 4 * P, xq[tg, c], 0, W, c == 0, c == NC - 1)
+
+        accs, psg = {}, {}
+
+        def p_open(tg, slot):
+            accs[tg, slot] = ps.tile([P, W], F32, name="bank")
+
+        def p_unit(tg, slot):
+            p_open(tg, slot)
+            for c in range(NC):
+                p_pass(accs[tg, slot], tg, slot, c)
+
+        def p_scale(tg, slot, on_vector=False):
+            g, k = divmod(slot, 4)
+            if (tg, g) not in psraw:
+                psraw[tg, g] = t4.tile([P, 4, W], BF16, name="t4", align_bytes=64)
+            dst, col = psraw[tg, g][:, k, :], s_cols[:, g, k : k + 1]
+            if on_vector:
+                nc.vector.tensor_scalar(out=dst, in0=accs[tg, slot][:], scalar1=col, scalar2=None, op0=ALU.mult)
+            else:
+                nc.scalar.activation(out=dst, in_=accs[tg, slot][:], func=ACT.Copy, scale=col)
+
+        def p_keep(tg, slot, on_vector=False):
+            g, k = divmod(slot, 4)
+            h0t[tg, slot] = h0tp.tile([P, W], F32, name="h0t")
+            dst, col = h0t[tg, slot][:], b_cols[:, g, k : k + 1]
+            if on_vector:
+                nc.vector.tensor_scalar(
+                    out=dst, in0=accs[tg, slot][:], scalar1=1.5, scalar2=col, op0=ALU.mult, op1=ALU.add
+                )
+            else:
+                nc.scalar.activation(out=dst, in_=accs[tg, slot][:], func=ACT.Identity, scale=1.5, bias=col)
+
+        def ps_group(tg, g):
+            psg[tg, g] = t4.tile([P, W, 4], BF16, name="t4", align_bytes=64)
+            nc.vector.tensor_copy(out=psg[tg, g][:], in_=psraw[tg, g][:].rearrange("p t n -> p n t"))
+
+        def ps_quant(tg, g):
+            quantize(psq[tg, g], 0, W, psg[tg, g][:].rearrange("p n t -> p (n t)"))
+
+        graw, gacc, gg = {}, {}, {}
+
+        def g_open(gi, k, jg):
+            gacc[gi, k, jg] = ps.tile([P, W], F32, name="bank")
+
+        def g_pass(gi, k, jg, c):
+            mx(gacc[gi, k, jg][:], wdq[gi, c], k * P, wq[jg, c], 0, W, c == 0, c == NC - 1)
+
+        def g_unit(gi, k, jg):
+            g_open(gi, k, jg)
+            for c in range(NC):
+                g_pass(gi, k, jg, c)
+
+        def g_out(gi, k, jg, on_vector=False):
+            if (gi, jg) not in graw:
+                graw[gi, jg] = t4.tile([P, 4, W], BF16, name="t4", align_bytes=64)
+            dst = graw[gi, jg][:, k, :].rearrange("p (m t) -> p m t", t=4)
+            src = gacc[gi, k, jg][:].rearrange("p (t m) -> p m t", t=4)
+            col = t_cols[:, gi, k : k + 1]
+            if on_vector:
+                nc.vector.tensor_scalar(out=dst, in0=src, scalar1=col, scalar2=None, op0=ALU.mult)
+            else:
+                nc.scalar.activation(out=dst, in_=src, func=ACT.Copy, scale=col)
+
+        def g_group(gi, jg):
+            gg[gi, jg] = t4.tile([P, W, 4], BF16, name="t4", align_bytes=64)
+            nc.vector.tensor_copy(out=gg[gi, jg][:], in_=graw[gi, jg][:].rearrange("p t n -> p n t"))
+
+        def g_quant(gi, jg):
+            quantize(gq[gi, jg], 0, W, gg[gi, jg][:].rearrange("p n t -> p (n t)"))
+
+        h0, hbank = {}, {}
+
+        def h_turn(tg, q, g):
+            bank = ps.tile([P, 4, P], F32, name="bank")
+            hbank[tg, q, g] = bank
+            for k in range(4):
+                nc.tensor.transpose(bank[:, k, :], h0t[tg, 4 * g + k][:, q * P : (q + 1) * P], ident[:])
+
+        def h_out(tg, q, g, on_vector=False):
+            if (tg, q) not in h0:
+                h0[tg, q] = h0p.tile([P, 2, W], F32, name="h0")
+            dst = h0[tg, q][:, g, :].rearrange("p (m t) -> p m t", t=4)
+            src = hbank[tg, q, g][:].rearrange("p t m -> p m t")
+            if on_vector:
+                nc.vector.tensor_copy(out=dst, in_=src)
+            else:
+                nc.scalar.copy(out=dst, in_=src)
+
+        outq, racc, hh = {}, {}, {}
+        out_v = out.rearrange("(a m t) (h q f) -> a m t h q f", a=2, t=4, h=2, q=2)
+
+        def r_side(tg, q, jg):
+            acc = ps.tile([P, W], F32, name="bank")
+            racc[tg, q, jg] = acc
+            for gi in range(2):
+                mx(acc[:], psq[tg, gi], q * P, gq[gi, jg], 0, W, gi == 0, gi == 1)
+
+        def r_side_sum(tg, q, jg):
+            side = h0[tg, q][:, jg, :]
+            nc.vector.scalar_tensor_tensor(
+                out=side, in0=racc[tg, q, jg][:], scalar=-0.5, in1=side, op0=ALU.mult, op1=ALU.add
+            )
+
+        def r_side_sort(tg, q):
+            for half in range(2):
+                if (tg, half) not in outq:
+                    outq[tg, half] = t8.tile([P, 4, 2, 256], F32, name="t8", align_bytes=64)
+            h = h0[tg, q]
+            for half in range(2):
+                o = outq[tg, half]
+                cols = slice(half * 256, half * 256 + 256)
+                nc.vector.tensor_tensor(out=o[:, q, 0, :], in0=h[:, 0, cols], in1=h[:, 1, cols], op=ALU.max)
+                nc.vector.tensor_tensor(out=o[:, q, 1, :], in0=h[:, 0, cols], in1=h[:, 1, cols], op=ALU.min)
+                nc.sync.dma_start(out=out_v[tg, :, q, :, half, :], in_=o[:, q, :, :])
+
+        def r_unit(tg, q, half):
+            acc = ps.tile([P, 2, 256], F32, name="bank")
+            racc[tg, q, half] = acc
+            for jg in range(2):
+                for gi in range(2):
+                    mx(acc[:, jg, :], psq[tg, gi], q * P, gq[gi, jg], half * 256, 256, gi == 0, gi == 1)
+
+        def r_sum(tg, q, half):
+            hh[tg, q, half] = hp.tile([P, 2, 256], F32, name="h")
+            nc.vector.scalar_tensor_tensor(
+                out=hh[tg, q, half][:],
+                in0=racc[tg, q, half][:],
+                scalar=-0.5,
+                in1=h0[tg, q][:, :, half * 256 : (half + 1) * 256],
+                op0=ALU.mult,
+                op1=ALU.add,
+            )
+
+        def r_sort(tg, q, half):
+            h = hh[tg, q, half]
+            if (tg, half) not in outq:
+                outq[tg, half] = t8.tile([P, 4, 2, 256], F32, name="t8", align_bytes=64)
+            o = outq[tg, half]
+            nc.vector.tensor_tensor(out=o[:, q, 0, :], in0=h[:, 0, :], in1=h[:, 1, :], op=ALU.max)
+            nc.vector.tensor_tensor(out=o[:, q, 1, :], in0=h[:, 0, :], in1=h[:, 1, :], op=ALU.min)
+            nc.sync.dma_start(out=out_v[tg, :, q, :, half, :], in_=o[:, q, :, :])
+
+        words_v = [out_words[tg].rearrange("p m t -> p (m t)").bitcast(I32).rearrange(
+            "p (h q f) -> p h q f", h=2, q=2) for tg in range(2)]
+        scales_v = [out_scales[tg].bitcast(I32).rearrange("r (h q f) -> r h q f", h=2, q=2) for tg in range(2)]
+
+        ob = {}
+
+        def o_group(tg, half, part, on_vector=False):
+            if (tg, half) not in ob:
+                ob[tg, half] = t4.tile([P, W, 4], BF16, name="t4", align_bytes=64)
+            dst = ob[tg, half][:, part * 256 : (part + 1) * 256, :]
+            src = outq[tg, half][:, :, part, :].rearrange("p t f -> p f t")
+            if on_vector:
+                nc.vector.tensor_copy(out=dst, in_=src)
+            else:
+                nc.scalar.copy(out=dst, in_=src)
+
+        def o_quant(tg, half):
+            oq = oqp.tile([P, W], U32, name="oq", align_bytes=64)
+            osc = oqp.tile([P, W], U8, name="osc", align_bytes=64)
+            quantize((oq, osc), 0, W, ob[tg, half][:].rearrange("p n t -> p (n t)"))
+            nc.sync.dma_start(
+                out=words_v[tg][:, :, half, :], in_=oq[:].bitcast(I32).rearrange("p (h f) -> p h f", h=2)
+            )
+            for quad in range(4):
+                nc.sync.dma_start(
+                    out=scales_v[tg][4 * quad : 4 * quad + 4, :, half, :],
+                    in_=osc[32 * quad : 32 * quad + 4, :].bitcast(I32).rearrange("r (h f) -> r h f", h=2),
+                )
+
+        with tc.manual_schedule():
+            w_group(0, 0, False)
+            w_group(0, 1, True)
+            wd_make(0, 0)
+            w_quant(0, 0)
+            wd_quant(0, 0)
+            x_turn(0, 0, 1)
+            wd_make(0, 1)
+            x_turn(0, 1, 1)
+            x_turn(0, 1, 0)
+            w_quant(0, 1)
+            x_out(0, 1, 1, False)
+            x_turn(0, 0, 0)
+            x_out(0, 1, 0, False)
+            wd_quant(0, 1)
+            g_open(0, 2, 0)
+            g_pass(0, 2, 0, 0)
+            g_open(0, 0, 0)
+            g_pass(0, 0, 0, 0)
+            x_out(0, 0, 0, False)
+            w_group(0, 2, False)
+            g_pass(0, 0, 0, 1)
+            x_out(0, 0, 1, False)
+            g_pass(0, 2, 0, 1)
+            g_open(0, 1, 0)
+            g_pass(0, 1, 0, 0)
+            w_group(0, 3, True)
+            x_quant(0, 0)
+            g_pass(0, 1, 0, 1)
+            wd_make(0, 2)
+            p_open(0, 2)
+            p_pass(accs[0, 2], 0, 2, 0)
+            p_open(0, 0)
+            p_pass(accs[0, 0], 0, 0, 0)
+            x_turn(0, 3, 0)
+            w_quant(0, 2)
+            x_turn(0, 2, 1)
+            x_out(0, 3, 0, False)
+            x_quant(0, 1)
+            x_turn(0, 2, 0)
+            x_out(0, 2, 1, False)
+            wd_make(0, 3)
+            x_turn(0, 3, 1)
+            x_out(0, 2, 0, False)
+            g_open(0, 3, 0)
+            g_pass(0, 3, 0, 0)
+            p_pass(accs[0, 2], 0, 2, 1)
+            x_out(0, 3, 1, False)
+            g_pass(0, 3, 0, 1)
+            wd_quant(0, 2)
+            p_open(0, 1)
+            p_pass(accs[0, 1], 0, 1, 0)
+            w_group(1, 1, True)
+            p_pass(accs[0, 0], 0, 0, 1)
+            x_quant(0, 2)
+            p_pass(accs[0, 1], 0, 1, 1)
+            g_pass(0, 1, 0, 2)
+            w_quant(0, 3)
+            g_pass(0, 0, 0, 2)
+            g_pass(0, 3, 0, 2)
+            wd_quant(0, 3)
+            p_open(0, 3)
+            p_pass(accs[0, 3], 0, 3, 0)
+            g_pass(0, 2, 0, 2)
+            w_group(1, 2, False)
+            p_pass(accs[0, 3], 0, 3, 1)
+            g_pass(0, 0, 0, 3)
+            w_group(1, 3, True)
+            p_pass(accs[0, 0], 0, 0, 2)
+            g_pass(0, 2, 0, 3)
+            p_pass(accs[0, 3], 0, 3, 2)
+            x_quant(0, 3)
+            g_pass(0, 1, 0, 3)
+            p_pass(accs[0, 1], 0, 1, 2)
+            p_pass(accs[0, 2], 0, 2, 2)
+            g_out(0, 0, 0, True)
+            p_pass(accs[0, 0], 0, 0, 3)
+            p_pass(accs[0, 3], 0, 3, 3)
+            w_group(1, 0, False)
+            x_turn(1, 0, 1)
+            g_out(0, 1, 0, False)
+            g_pass(0, 3, 0, 3)
+            p_pass(accs[0, 2], 0, 2, 3)
+            p_scale(0, 0, False)
+            p_pass(accs[0, 1], 0, 1, 3)
+            x_out(1, 0, 1, True)
+            x_turn(1, 1, 1)
+            g_out(0, 3, 0, False)
+            w_quant(1, 0)
+            x_turn(1, 1, 0)
+            x_out(1, 1, 1, False)
+            p_keep(0, 0, True)
+            x_turn(1, 3, 1)
+            x_out(1, 1, 0, False)
+            w_quant(1, 1)
+            p_open(0, 6)
+            p_pass(accs[0, 6], 0, 6, 0)
+            x_turn(1, 2, 0)
+            g_out(0, 2, 0, False)
+            w_quant(1, 2)
+            p_pass(accs[0, 6], 0, 6, 1)
+            p_scale(0, 2, False)
+            g_open(0, 0, 1)
+            g_pass(0, 0, 1, 0)
+            x_out(1, 3, 1, True)
+            g_open(0, 3, 1)
+            g_pass(0, 3, 1, 0)
+            p_pass(accs[0, 6], 0, 6, 2)
+            p_keep(0, 2, False)
+            wd_make(1, 3)
+            g_open(0, 2, 1)
+            g_pass(0, 2, 1, 0)
+            g_pass(0, 3, 1, 1)
+            p_scale(0, 3, False)
+            g_pass(0, 2, 1, 1)
+            g_pass(0, 3, 1, 2)
+            w_quant(1, 3)
+            x_out(1, 2, 0, False)
+            g_pass(0, 0, 1, 1)
+            p_open(0, 7)
+            p_pass(accs[0, 7], 0, 7, 0)
+            wd_make(1, 0)
+            p_keep(0, 3, False)
+            p_open(0, 4)
+            p_pass(accs[0, 4], 0, 4, 0)
+            p_pass(accs[0, 7], 0, 7, 1)
+            p_scale(0, 1, False)
+            p_pass(accs[0, 4], 0, 4, 1)
+            g_open(0, 1, 1)
+            g_pass(0, 1, 1, 0)
+            x_quant(1, 1)
+            p_pass(accs[0, 4], 0, 4, 2)
+            p_keep(0, 1, False)
+            g_pass(0, 0, 1, 2)
+            p_pass(accs[0, 4], 0, 4, 3)
+            wd_quant(1, 0)
+            g_pass(0, 0, 1, 3)
+            g_pass(0, 1, 1, 1)
+            p_scale(0, 4, False)
+            wd_make(1, 1)
+            g_pass(0, 3, 1, 3)
+            p_pass(accs[0, 7], 0, 7, 2)
+            g_out(0, 0, 1, False)
+            x_turn(1, 0, 0)
+            g_out(0, 3, 1, False)
+            wd_make(1, 2)
+            p_pass(accs[0, 7], 0, 7, 3)
+            p_pass(accs[0, 6], 0, 6, 3)
+            p_keep(0, 4, False)
+            g_pass(0, 1, 1, 2)
+            h_turn(0, 3, 0)
+            p_scale(0, 7, True)
+            x_turn(1, 3, 0)
+            h_out(0, 3, 0, False)
+            x_out(1, 0, 0, True)
+            g_open(1, 2, 1)
+            g_pass(1, 2, 1, 0)
+            g_pass(0, 2, 1, 2)
+            x_out(1, 3, 0, False)
+            wd_quant(1, 2)
+            x_turn(1, 2, 1)
+            p_scale(0, 6, False)
+            wd_quant(1, 1)
+            g_open(1, 1, 1)
+            g_pass(1, 1, 1, 0)
+            g_pass(0, 2, 1, 3)
+            x_out(1, 2, 1, False)
+            x_quant(1, 0)
+            p_open(0, 5)
+            p_pass(accs[0, 5], 0, 5, 0)
+            g_pass(0, 1, 1, 3)
+            p_keep(0, 7, False)
+            p_pass(accs[0, 5], 0, 5, 1)
+            wd_quant(1, 3)
+            g_pass(1, 1, 1, 1)
+            g_out(0, 2, 1, False)
+            g_open(1, 0, 1)
+            g_pass(1, 0, 1, 0)
+            x_quant(1, 2)
+            g_pass(1, 1, 1, 2)
+            g_out(0, 1, 1, False)
+            g_open(1, 0, 0)
+            g_pass(1, 0, 0, 0)
+            x_quant(1, 3)
+            g_pass(1, 2, 1, 1)
+            g_pass(1, 1, 1, 3)
+            p_keep(0, 6, True)
+            g_pass(1, 2, 1, 2)
+            g_pass(1, 0, 0, 1)
+            g_out(1, 1, 1, True)
+            g_open(1, 3, 1)
+            g_pass(1, 3, 1, 0)
+            p_pass(accs[0, 5], 0, 5, 2)
+            g_open(1, 3, 0)
+            g_pass(1, 3, 0, 0)
+            g_group(0, 0)
+            p_open(1, 6)
+            p_pass(accs[1, 6], 1, 6, 0)
+            g_pass(1, 0, 0, 2)
+            g_pass(1, 3, 1, 1)
+            p_pass(accs[1, 6], 1, 6, 1)
+            g_pass(1, 3, 1, 2)
+            ps_group(0, 0)
+            g_pass(1, 2, 1, 3)
+            p_pass(accs[0, 5], 0, 5, 3)
+            g_open(1, 1, 0)
+            g_pass(1, 1, 0, 0)
+            g_pass(1, 3, 1, 3)
+            p_scale(0, 5, False)
+            g_group(0, 1)
+            g_pass(1, 0, 1, 1)
+            g_pass(1, 0, 0, 3)
+            p_keep(0, 5, False)
+            g_pass(1, 0, 1, 2)
+            g_pass(1, 3, 0, 1)
+            g_pass(1, 0, 1, 3)
+            g_out(1, 0, 0, False)
+            g_quant(0, 0)
+            g_pass(1, 1, 0, 1)
+            p_open(1, 4)
+            p_pass(accs[1, 4], 1, 4, 0)
+            g_out(1, 2, 1, False)
+            g_pass(1, 3, 0, 2)
+            ps_group(0, 1)
+            p_open(1, 5)
+            p_pass(accs[1, 5], 1, 5, 0)
+            g_out(1, 0, 1, False)
+            p_pass(accs[1, 6], 1, 6, 2)
+            p_pass(accs[1, 4], 1, 4, 1)
+            g_out(1, 3, 1, False)
+            g_open(1, 2, 0)
+            g_pass(1, 2, 0, 0)
+            h_turn(0, 2, 0)
+            ps_quant(0, 0)
+            g_pass(1, 1, 0, 2)
+            g_group(1, 1)
+            p_pass(accs[1, 6], 1, 6, 3)
+            p_pass(accs[1, 4], 1, 4, 2)
+            g_pass(1, 2, 0, 1)
+            p_pass(accs[1, 5], 1, 5, 1)
+            g_pass(1, 3, 0, 3)
+            p_open(1, 7)
+            p_pass(accs[1, 7], 1, 7, 0)
+            g_quant(1, 1)
+            p_pass(accs[1, 4], 1, 4, 3)
+            g_out(1, 3, 0, False)
+            g_pass(1, 1, 0, 3)
+            h_out(0, 2, 0, True)
+            p_pass(accs[1, 7], 1, 7, 1)
+            p_scale(1, 6, False)
+            g_pass(1, 2, 0, 2)
+            g_quant(0, 1)
+            p_pass(accs[1, 7], 1, 7, 2)
+            p_scale(1, 4, False)
+            g_pass(1, 2, 0, 3)
+            p_pass(accs[1, 5], 1, 5, 2)
+            ps_quant(0, 1)
+            p_open(1, 2)
+            p_pass(accs[1, 2], 1, 2, 0)
+            p_keep(1, 4, False)
+            h_turn(0, 2, 1)
+            g_out(1, 1, 0, True)
+            p_pass(accs[1, 5], 1, 5, 3)
+            g_out(1, 2, 0, False)
+            p_keep(1, 6, True)
+            p_open(1, 3)
+            p_pass(accs[1, 3], 1, 3, 0)
+            p_open(1, 0)
+            p_pass(accs[1, 0], 1, 0, 0)
+            p_scale(1, 5, False)
+            p_pass(accs[1, 7], 1, 7, 3)
+            g_group(1, 0)
+            p_pass(accs[1, 2], 1, 2, 1)
+            p_pass(accs[1, 0], 1, 0, 1)
+            p_scale(1, 7, False)
+            p_pass(accs[1, 3], 1, 3, 1)
+            p_pass(accs[1, 2], 1, 2, 2)
+            h_out(0, 2, 1, False)
+            p_pass(accs[1, 0], 1, 0, 2)
+            ps_group(1, 1)
+            p_pass(accs[1, 2], 1, 2, 3)
+            p_keep(1, 7, False)
+            p_pass(accs[1, 3], 1, 3, 2)
+            r_side(0, 2, 1)
+            p_scale(1, 2, False)
+            g_quant(1, 0)
+            p_pass(accs[1, 0], 1, 0, 3)
+            p_keep(1, 5, False)
+            p_pass(accs[1, 3], 1, 3, 3)
+            p_open(1, 1)
+            p_pass(accs[1, 1], 1, 1, 0)
+            ps_quant(1, 1)
+            r_side(0, 2, 0)
+            p_scale(1, 3, False)
+            r_side_sum(0, 2, 1)
+            p_pass(accs[1, 1], 1, 1, 1)
+            p_keep(1, 3, False)
+            r_side(0, 3, 0)
+            r_side_sum(0, 2, 0)
+            p_scale(1, 0, False)
+            p_pass(accs[1, 1], 1, 1, 2)
+            h_turn(0, 1, 1)
+            r_side_sum(0, 3, 0)
+            p_keep(1, 2, False)
+            p_pass(accs[1, 1], 1, 1, 3)
+            r_side_sort(0, 2)
+            h_turn(0, 0, 0)
+            p_scale(1, 1, False)
+            h_turn(0, 3, 1)
+            r_side(0, 3, 1)
+            h_out(0, 3, 1, False)
+            ps_group(1, 0)
+            h_turn(1, 0, 1)
+            h_turn(0, 0, 1)
+            h_out(1, 0, 1, False)
+            r_side(0, 0, 0)
+            r_side_sum(0, 3, 1)
+            h_out(0, 1, 1, False)
+            r_side(0, 1, 1)
+            ps_quant(1, 0)
+            h_out(0, 0, 0, False)
+            h_turn(1, 2, 1)
+            r_side(0, 1, 0)
+            p_keep(1, 1, False)
+            r_side_sort(0, 3)
+            r_side(0, 0, 1)
+            p_keep(1, 0, False)
+            h_turn(0, 1, 0)
+            h_out(0, 0, 1, False)
+            r_side_sum(0, 1, 1)
+            r_unit(1, 3, 0)
+            h_out(0, 1, 0, False)
+            r_side_sum(0, 0, 0)
+            h_turn(1, 0, 0)
+            h_out(1, 2, 1, False)
+            h_turn(1, 3, 0)
+            r_side_sum(0, 0, 1)
+            h_turn(1, 1, 0)
+            r_side_sum(0, 1, 0)
+            h_out(1, 3, 0, False)
+            h_turn(1, 2, 0)
+            h_turn(1, 1, 1)
+            r_side_sort(0, 0)
+            h_turn(1, 3, 1)
+            r_unit(1, 2, 1)
+            h_out(1, 3, 1, False)
+            r_side_sort(0, 1)
+            r_unit(1, 0, 1)
+            h_out(1, 0, 0, False)
+            r_unit(1, 1, 1)
+            h_out(1, 1, 0, False)
+            r_unit(1, 1, 0)
+            r_sum(1, 3, 0)
+            h_out(1, 1, 1, False)
+            r_unit(1, 0, 0)
+            r_sum(1, 0, 1)
+            h_out(1, 2, 0, False)
+            r_unit(1, 3, 1)
+            r_sum(1, 1, 0)
+            o_group(0, 0, 0, False)
+            r_unit(1, 2, 0)
+            r_sum(1, 1, 1)
+            r_sort(1, 0, 1)
+            o_group(0, 0, 1, False)
+            r_sort(1, 1, 1)
+            r_sort(1, 1, 0)
+            o_group(0, 1, 0, False)
+            r_sum(1, 3, 1)
+            r_sum(1, 2, 1)
+            o_group(0, 1, 1, False)
+            r_sort(1, 3, 1)
+            r_sort(1, 2, 1)
+            r_sum(1, 0, 0)
+            o_group(1, 1, 0, False)
+            r_sum(1, 2, 0)
+            r_sort(1, 3, 0)
+            o_group(1, 1, 1, False)
+            r_sort(1, 0, 0)
+            r_sort(1, 2, 0)
+            o_quant(0, 1)
+            o_group(1, 0, 1, False)
+            o_group(1, 0, 0, True)
+            o_quant(1, 1)
+            o_quant(0, 0)
+            o_quant(1, 0)

@@ -18,21 +18,17 @@ ACT = mybir.ActivationFunctionType
 P = 128
 W = 512
 NC = D // W
-T4_BUFS = 15
-H0T_BUFS = 14
 
 
 def tile_bjorckmaxmindense_x1_kernel(tc, x, w, d, s, t, b, out, out_words, out_scales):
     nc = tc.nc
     with ExitStack() as ctx:
         const = ctx.enter_context(tc.tile_pool(name="const", bufs=1))
-        t8 = ctx.enter_context(tc.tile_pool(name="t8", bufs=4))
-        t4 = ctx.enter_context(tc.tile_pool(name="t4", bufs=T4_BUFS))
+        t8 = ctx.enter_context(tc.tile_pool(name="t8", bufs=7))
+        t4 = ctx.enter_context(tc.tile_pool(name="t4", bufs=18))
         keep = ctx.enter_context(tc.tile_pool(name="keep", bufs=1))
-        h0tp = ctx.enter_context(tc.tile_pool(name="h0tp", bufs=H0T_BUFS))
-        h0p = ctx.enter_context(tc.tile_pool(name="h0p", bufs=5))
-        hp = ctx.enter_context(tc.tile_pool(name="hp", bufs=4))
-        oqp = ctx.enter_context(tc.tile_pool(name="oqp", bufs=2))
+        hp = ctx.enter_context(tc.tile_pool(name="hp", bufs=3))
+        oqp = ctx.enter_context(tc.tile_pool(name="oqp", bufs=4))
         ps = ctx.enter_context(tc.psum_pool(name="ps", bufs=8))
 
         d_cols = const.tile([P, NC, 4], BF16)
@@ -182,18 +178,24 @@ def tile_bjorckmaxmindense_x1_kernel(tc, x, w, d, s, t, b, out, out_words, out_s
 
         def p_keep(tg, slot, on_vector=False):
             g, k = divmod(slot, 4)
-            h0t[tg, slot] = h0tp.tile([P, W], F32, name="h0t")
-            dst, col = h0t[tg, slot][:], b_cols[:, g, k : k + 1]
+            if (tg, g) not in h0t:
+                h0t[tg, g] = t8.tile([P, 4, 4, P], F32, name="t8", align_bytes=64)
+            dst, col = h0t[tg, g][:, :, k, :], b_cols[:, g, k : k + 1]
+            src = accs[tg, slot][:].rearrange("p (q n) -> p q n", q=4)
             if on_vector:
-                nc.vector.tensor_scalar(
-                    out=dst, in0=accs[tg, slot][:], scalar1=1.5, scalar2=col, op0=ALU.mult, op1=ALU.add
+                nc.vector.tensor_scalar(out=dst, in0=src, scalar1=1.5, scalar2=col, op0=ALU.mult, op1=ALU.add)
+            else:
+                nc.scalar.activation(out=dst, in_=src, func=ACT.Identity, scale=1.5, bias=col)
+
+        def ps_group(tg, g, on_gpsimd=False):
+            psg[tg, g] = t4.tile([P, W, 4], BF16, name="t4", align_bytes=64)
+            src = psraw[tg, g][:].rearrange("p t n -> p n t")
+            if on_gpsimd:
+                nc.gpsimd.tensor_scalar(
+                    out=psg[tg, g][:], in0=src, scalar1=1.0, scalar2=0.0, op0=ALU.mult, op1=ALU.add
                 )
             else:
-                nc.scalar.activation(out=dst, in_=accs[tg, slot][:], func=ACT.Identity, scale=1.5, bias=col)
-
-        def ps_group(tg, g):
-            psg[tg, g] = t4.tile([P, W, 4], BF16, name="t4", align_bytes=64)
-            nc.vector.tensor_copy(out=psg[tg, g][:], in_=psraw[tg, g][:].rearrange("p t n -> p n t"))
+                nc.vector.tensor_copy(out=psg[tg, g][:], in_=src)
 
         def ps_quant(tg, g):
             quantize(psq[tg, g], 0, W, psg[tg, g][:].rearrange("p n t -> p (n t)"))
@@ -214,8 +216,7 @@ def tile_bjorckmaxmindense_x1_kernel(tc, x, w, d, s, t, b, out, out_words, out_s
         def g_out(gi, k, jg, on_vector=False):
             if (gi, jg) not in graw:
                 graw[gi, jg] = t4.tile([P, 4, W], BF16, name="t4", align_bytes=64)
-            dst = graw[gi, jg][:, k, :].rearrange("p (m t) -> p m t", t=4)
-            src = gacc[gi, k, jg][:].rearrange("p (t m) -> p m t", t=4)
+            dst, src = graw[gi, jg][:, k, :], gacc[gi, k, jg][:]
             col = t_cols[:, gi, k : k + 1]
             if on_vector:
                 nc.vector.tensor_scalar(out=dst, in0=src, scalar1=col, scalar2=None, op0=ALU.mult)
@@ -229,105 +230,85 @@ def tile_bjorckmaxmindense_x1_kernel(tc, x, w, d, s, t, b, out, out_words, out_s
         def g_quant(gi, jg):
             quantize(gq[gi, jg], 0, W, gg[gi, jg][:].rearrange("p n t -> p (n t)"))
 
-        h0, hbank = {}, {}
+        hbank, hr, racc, outs = {}, {}, {}, {}
+        out_v = out.rearrange("(a m t) (h f) -> a m t h f", a=2, t=4, h=2)
+
+        def r_unit(tg, q, g):
+            acc = ps.tile([P, 4, P], F32, name="bank")
+            racc[tg, q, g] = acc
+            for k in range(4):
+                for gi in range(2):
+                    mx(acc[:, k, :], gq[gi, g], k * P, psq[tg, gi], q * P, P, gi == 0, gi == 1)
+
+        def r_sum(tg, q, g):
+            h = h0t[tg, g][:, q, :, :]
+            nc.vector.scalar_tensor_tensor(
+                out=h, in0=racc[tg, q, g][:], scalar=-0.5, in1=h, op0=ALU.mult, op1=ALU.add
+            )
+
+        rcopy = {}
+
+        def r_copy(tg, q, g):
+            rcopy[tg, q, g] = hp.tile([P, 4, P], F32, name="rc")
+            nc.scalar.activation(out=rcopy[tg, q, g][:], in_=racc[tg, q, g][:], func=ACT.Copy, scale=-0.5)
+
+        def r_add(tg, q, g):
+            h = h0t[tg, g][:, q, :, :]
+            nc.gpsimd.tensor_tensor(out=h, in0=h, in1=rcopy[tg, q, g][:], op=ALU.add)
 
         def h_turn(tg, q, g):
             bank = ps.tile([P, 4, P], F32, name="bank")
             hbank[tg, q, g] = bank
             for k in range(4):
-                nc.tensor.transpose(bank[:, k, :], h0t[tg, 4 * g + k][:, q * P : (q + 1) * P], ident[:])
+                nc.tensor.transpose(bank[:, k, :], h0t[tg, g][:, q, k, :], ident[:])
 
-        def h_out(tg, q, g, on_vector=False):
-            if (tg, q) not in h0:
-                h0[tg, q] = h0p.tile([P, 2, W], F32, name="h0")
-            dst = h0[tg, q][:, g, :].rearrange("p (m t) -> p m t", t=4)
-            src = hbank[tg, q, g][:].rearrange("p t m -> p m t")
-            if on_vector:
-                nc.vector.tensor_copy(out=dst, in_=src)
-            else:
-                nc.scalar.copy(out=dst, in_=src)
-
-        outq, racc, hh = {}, {}, {}
-        out_v = out.rearrange("(a m t) (h q f) -> a m t h q f", a=2, t=4, h=2, q=2)
-
-        def r_side(tg, q, jg):
-            acc = ps.tile([P, W], F32, name="bank")
-            racc[tg, q, jg] = acc
-            for gi in range(2):
-                mx(acc[:], psq[tg, gi], q * P, gq[gi, jg], 0, W, gi == 0, gi == 1)
-
-        def r_side_sum(tg, q, jg):
-            side = h0[tg, q][:, jg, :]
-            nc.vector.scalar_tensor_tensor(
-                out=side, in0=racc[tg, q, jg][:], scalar=-0.5, in1=side, op0=ALU.mult, op1=ALU.add
+        def h_out(tg, q):
+            hr[tg, q] = hp.tile([P, W], F32, name="hr")
+            nc.scalar.copy(
+                out=hr[tg, q][:].rearrange("p (m t) -> p m t", t=4),
+                in_=hbank[tg, q, 1][:].rearrange("p t m -> p m t"),
             )
 
-        def r_side_sort(tg, q):
-            for half in range(2):
-                if (tg, half) not in outq:
-                    outq[tg, half] = t8.tile([P, 4, 2, 256], F32, name="t8", align_bytes=64)
-            h = h0[tg, q]
-            for half in range(2):
-                o = outq[tg, half]
-                cols = slice(half * 256, half * 256 + 256)
-                nc.vector.tensor_tensor(out=o[:, q, 0, :], in0=h[:, 0, cols], in1=h[:, 1, cols], op=ALU.max)
-                nc.vector.tensor_tensor(out=o[:, q, 1, :], in0=h[:, 0, cols], in1=h[:, 1, cols], op=ALU.min)
-                nc.sync.dma_start(out=out_v[tg, :, q, :, half, :], in_=o[:, q, :, :])
-
-        def r_unit(tg, q, half):
-            acc = ps.tile([P, 2, 256], F32, name="bank")
-            racc[tg, q, half] = acc
-            for jg in range(2):
-                for gi in range(2):
-                    mx(acc[:, jg, :], psq[tg, gi], q * P, gq[gi, jg], half * 256, 256, gi == 0, gi == 1)
-
-        def r_sum(tg, q, half):
-            hh[tg, q, half] = hp.tile([P, 2, 256], F32, name="h")
-            nc.vector.scalar_tensor_tensor(
-                out=hh[tg, q, half][:],
-                in0=racc[tg, q, half][:],
-                scalar=-0.5,
-                in1=h0[tg, q][:, :, half * 256 : (half + 1) * 256],
-                op0=ALU.mult,
-                op1=ALU.add,
+        def r_pick(tg, q, side):
+            if (tg, side) not in outs:
+                outs[tg, side] = t8.tile([P, 4, W], F32, name="t8", align_bytes=64)
+            o = outs[tg, side]
+            nc.vector.tensor_tensor(
+                out=o[:, q, :].rearrange("p (m t) -> p m t", t=4),
+                in0=hbank[tg, q, 0][:].rearrange("p t m -> p m t"),
+                in1=hr[tg, q][:].rearrange("p (m t) -> p m t", t=4),
+                op=ALU.min if side else ALU.max,
             )
+            nc.sync.dma_start(out=out_v[tg, :, q, side, :], in_=o[:, q, :])
 
-        def r_sort(tg, q, half):
-            h = hh[tg, q, half]
-            if (tg, half) not in outq:
-                outq[tg, half] = t8.tile([P, 4, 2, 256], F32, name="t8", align_bytes=64)
-            o = outq[tg, half]
-            nc.vector.tensor_tensor(out=o[:, q, 0, :], in0=h[:, 0, :], in1=h[:, 1, :], op=ALU.max)
-            nc.vector.tensor_tensor(out=o[:, q, 1, :], in0=h[:, 0, :], in1=h[:, 1, :], op=ALU.min)
-            nc.sync.dma_start(out=out_v[tg, :, q, :, half, :], in_=o[:, q, :, :])
-
-        words_v = [out_words[tg].rearrange("p m t -> p (m t)").bitcast(I32).rearrange(
-            "p (h q f) -> p h q f", h=2, q=2) for tg in range(2)]
-        scales_v = [out_scales[tg].bitcast(I32).rearrange("r (h q f) -> r h q f", h=2, q=2) for tg in range(2)]
-
+        words_v = [out_words[tg].rearrange("p m t -> p (m t)").bitcast(I32) for tg in range(2)]
+        scales_v = [out_scales[tg].bitcast(I32) for tg in range(2)]
         ob = {}
 
-        def o_group(tg, half, part, on_vector=False):
-            if (tg, half) not in ob:
-                ob[tg, half] = t4.tile([P, W, 4], BF16, name="t4", align_bytes=64)
-            dst = ob[tg, half][:, part * 256 : (part + 1) * 256, :]
-            src = outq[tg, half][:, :, part, :].rearrange("p t f -> p f t")
-            if on_vector:
+        def o_group(tg, side, half, eng):
+            if (tg, side) not in ob:
+                ob[tg, side] = t4.tile([P, W, 4], BF16, name="t4", align_bytes=64)
+            cols = slice(half * 256, half * 256 + 256)
+            dst = ob[tg, side][:, cols, :]
+            src = outs[tg, side][:, :, cols].rearrange("p t f -> p f t")
+            if eng == "v":
                 nc.vector.tensor_copy(out=dst, in_=src)
-            else:
+            elif eng == "s":
                 nc.scalar.copy(out=dst, in_=src)
+            else:
+                nc.gpsimd.tensor_scalar(
+                    out=dst, in0=src, scalar1=1.0, scalar2=0.0, op0=ALU.mult, op1=ALU.add
+                )
 
-        def o_quant(tg, half):
+        def o_quant(tg, side):
             oq = oqp.tile([P, W], U32, name="oq", align_bytes=64)
             osc = oqp.tile([P, W], U8, name="osc", align_bytes=64)
-            quantize((oq, osc), 0, W, ob[tg, half][:].rearrange("p n t -> p (n t)"))
-            nc.sync.dma_start(
-                out=words_v[tg][:, :, half, :], in_=oq[:].bitcast(I32).rearrange("p (h f) -> p h f", h=2)
-            )
+            quantize((oq, osc), 0, W, ob[tg, side][:].rearrange("p n t -> p (n t)"))
+            nc.sync.dma_start(out=words_v[tg][:, side * W : side * W + W], in_=oq[:].bitcast(I32))
             for quad in range(4):
                 nc.sync.dma_start(
-                    out=scales_v[tg][4 * quad : 4 * quad + 4, :, half, :],
-                    in_=osc[32 * quad : 32 * quad + 4, :].bitcast(I32).rearrange("r (h f) -> r h f", h=2),
+                    out=scales_v[tg][4 * quad : 4 * quad + 4, side * P : side * P + P],
+                    in_=osc[32 * quad : 32 * quad + 4, :].bitcast(I32),
                 )
 
         with tc.manual_schedule():
@@ -336,382 +317,290 @@ def tile_bjorckmaxmindense_x1_kernel(tc, x, w, d, s, t, b, out, out_words, out_s
             wd_make(0, 0)
             w_quant(0, 0)
             wd_quant(0, 0)
-            x_turn(0, 0, 1)
-            wd_make(0, 1)
-            x_turn(0, 1, 1)
-            x_turn(0, 1, 0)
-            w_quant(0, 1)
-            x_out(0, 1, 1, False)
             x_turn(0, 0, 0)
-            x_out(0, 1, 0, False)
-            wd_quant(0, 1)
-            g_open(0, 2, 0)
-            g_pass(0, 2, 0, 0)
-            g_open(0, 0, 0)
-            g_pass(0, 0, 0, 0)
+            wd_make(0, 1)
+            x_turn(0, 0, 1)
             x_out(0, 0, 0, False)
-            w_group(0, 2, False)
-            g_pass(0, 0, 0, 1)
-            x_out(0, 0, 1, False)
-            g_pass(0, 2, 0, 1)
             g_open(0, 1, 0)
             g_pass(0, 1, 0, 0)
-            w_group(0, 3, True)
-            x_quant(0, 0)
-            g_pass(0, 1, 0, 1)
-            wd_make(0, 2)
-            p_open(0, 2)
-            p_pass(accs[0, 2], 0, 2, 0)
-            p_open(0, 0)
-            p_pass(accs[0, 0], 0, 0, 0)
-            x_turn(0, 3, 0)
-            w_quant(0, 2)
-            x_turn(0, 2, 1)
-            x_out(0, 3, 0, False)
-            x_quant(0, 1)
-            x_turn(0, 2, 0)
-            x_out(0, 2, 1, False)
-            wd_make(0, 3)
-            x_turn(0, 3, 1)
-            x_out(0, 2, 0, False)
+            w_quant(0, 1)
+            x_out(0, 0, 1, False)
             g_open(0, 3, 0)
             g_pass(0, 3, 0, 0)
-            p_pass(accs[0, 2], 0, 2, 1)
-            x_out(0, 3, 1, False)
-            g_pass(0, 3, 0, 1)
-            wd_quant(0, 2)
+            g_open(0, 0, 0)
+            g_pass(0, 0, 0, 0)
+            w_group(0, 2, True)
+            wd_quant(0, 1)
+            x_turn(0, 1, 0)
+            x_quant(0, 0)
+            g_open(0, 2, 0)
+            g_pass(0, 2, 0, 0)
+            g_pass(0, 1, 0, 1)
+            w_group(0, 3, False)
             p_open(0, 1)
             p_pass(accs[0, 1], 0, 1, 0)
-            w_group(1, 1, True)
-            p_pass(accs[0, 0], 0, 0, 1)
-            x_quant(0, 2)
-            p_pass(accs[0, 1], 0, 1, 1)
-            g_pass(0, 1, 0, 2)
-            w_quant(0, 3)
-            g_pass(0, 0, 0, 2)
+            g_pass(0, 0, 0, 1)
+            g_pass(0, 2, 0, 1)
+            g_pass(0, 3, 0, 1)
+            x_out(0, 1, 0, False)
+            x_turn(0, 1, 1)
+            wd_make(0, 2)
+            x_turn(0, 3, 0)
+            x_out(0, 1, 1, False)
+            x_turn(0, 3, 1)
+            w_quant(0, 2)
+            x_out(0, 3, 0, False)
+            x_turn(0, 2, 0)
+            wd_quant(0, 2)
+            x_out(0, 3, 1, False)
+            x_turn(0, 2, 1)
+            x_quant(0, 1)
+            x_out(0, 2, 0, False)
+            p_open(0, 2)
+            p_pass(accs[0, 2], 0, 2, 0)
+            wd_make(0, 3)
             g_pass(0, 3, 0, 2)
-            wd_quant(0, 3)
+            x_out(0, 2, 1, False)
             p_open(0, 3)
             p_pass(accs[0, 3], 0, 3, 0)
             g_pass(0, 2, 0, 2)
-            w_group(1, 2, False)
+            w_group(1, 1, True)
+            g_pass(0, 1, 0, 2)
+            x_quant(0, 2)
             p_pass(accs[0, 3], 0, 3, 1)
-            g_pass(0, 0, 0, 3)
-            w_group(1, 3, True)
-            p_pass(accs[0, 0], 0, 0, 2)
-            g_pass(0, 2, 0, 3)
-            p_pass(accs[0, 3], 0, 3, 2)
-            x_quant(0, 3)
-            g_pass(0, 1, 0, 3)
+            p_pass(accs[0, 1], 0, 1, 1)
+            p_open(0, 0)
+            p_pass(accs[0, 0], 0, 0, 0)
+            wd_quant(0, 3)
+            p_pass(accs[0, 0], 0, 0, 1)
             p_pass(accs[0, 1], 0, 1, 2)
-            p_pass(accs[0, 2], 0, 2, 2)
-            g_out(0, 0, 0, True)
-            p_pass(accs[0, 0], 0, 0, 3)
-            p_pass(accs[0, 3], 0, 3, 3)
-            w_group(1, 0, False)
-            x_turn(1, 0, 1)
-            g_out(0, 1, 0, False)
-            g_pass(0, 3, 0, 3)
-            p_pass(accs[0, 2], 0, 2, 3)
-            p_scale(0, 0, False)
+            w_quant(0, 3)
+            p_pass(accs[0, 3], 0, 3, 2)
+            g_pass(0, 0, 0, 2)
+            x_quant(0, 3)
+            p_pass(accs[0, 0], 0, 0, 2)
+            w_group(1, 3, True)
+            p_pass(accs[0, 2], 0, 2, 1)
+            w_group(1, 2, False)
+            g_pass(0, 2, 0, 3)
             p_pass(accs[0, 1], 0, 1, 3)
-            x_out(1, 0, 1, True)
-            x_turn(1, 1, 1)
+            g_pass(0, 3, 0, 3)
+            g_pass(0, 1, 0, 3)
+            p_pass(accs[0, 0], 0, 0, 3)
+            g_out(0, 2, 0, True)
+            g_pass(0, 0, 0, 3)
+            p_pass(accs[0, 3], 0, 3, 3)
+            g_out(0, 1, 0, True)
+            p_pass(accs[0, 2], 0, 2, 2)
             g_out(0, 3, 0, False)
-            w_quant(1, 0)
-            x_turn(1, 1, 0)
-            x_out(1, 1, 1, False)
-            p_keep(0, 0, True)
-            x_turn(1, 3, 1)
-            x_out(1, 1, 0, False)
-            w_quant(1, 1)
-            p_open(0, 6)
-            p_pass(accs[0, 6], 0, 6, 0)
-            x_turn(1, 2, 0)
-            g_out(0, 2, 0, False)
-            w_quant(1, 2)
-            p_pass(accs[0, 6], 0, 6, 1)
-            p_scale(0, 2, False)
-            g_open(0, 0, 1)
-            g_pass(0, 0, 1, 0)
-            x_out(1, 3, 1, True)
-            g_open(0, 3, 1)
-            g_pass(0, 3, 1, 0)
-            p_pass(accs[0, 6], 0, 6, 2)
-            p_keep(0, 2, False)
-            wd_make(1, 3)
-            g_open(0, 2, 1)
-            g_pass(0, 2, 1, 0)
-            g_pass(0, 3, 1, 1)
-            p_scale(0, 3, False)
-            g_pass(0, 2, 1, 1)
-            g_pass(0, 3, 1, 2)
+            x_turn(1, 0, 1)
             w_quant(1, 3)
-            x_out(1, 2, 0, False)
-            g_pass(0, 0, 1, 1)
-            p_open(0, 7)
-            p_pass(accs[0, 7], 0, 7, 0)
-            wd_make(1, 0)
-            p_keep(0, 3, False)
-            p_open(0, 4)
-            p_pass(accs[0, 4], 0, 4, 0)
-            p_pass(accs[0, 7], 0, 7, 1)
-            p_scale(0, 1, False)
-            p_pass(accs[0, 4], 0, 4, 1)
-            g_open(0, 1, 1)
-            g_pass(0, 1, 1, 0)
-            x_quant(1, 1)
-            p_pass(accs[0, 4], 0, 4, 2)
-            p_keep(0, 1, False)
-            g_pass(0, 0, 1, 2)
-            p_pass(accs[0, 4], 0, 4, 3)
-            wd_quant(1, 0)
-            g_pass(0, 0, 1, 3)
-            g_pass(0, 1, 1, 1)
-            p_scale(0, 4, False)
-            wd_make(1, 1)
-            g_pass(0, 3, 1, 3)
-            p_pass(accs[0, 7], 0, 7, 2)
-            g_out(0, 0, 1, False)
+            g_out(0, 0, 0, False)
             x_turn(1, 0, 0)
-            g_out(0, 3, 1, False)
-            wd_make(1, 2)
-            p_pass(accs[0, 7], 0, 7, 3)
-            p_pass(accs[0, 6], 0, 6, 3)
-            p_keep(0, 4, False)
-            g_pass(0, 1, 1, 2)
-            h_turn(0, 3, 0)
-            p_scale(0, 7, True)
-            x_turn(1, 3, 0)
-            h_out(0, 3, 0, False)
-            x_out(1, 0, 0, True)
-            g_open(1, 2, 1)
-            g_pass(1, 2, 1, 0)
-            g_pass(0, 2, 1, 2)
-            x_out(1, 3, 0, False)
-            wd_quant(1, 2)
+            w_quant(1, 2)
+            x_out(1, 0, 1, False)
+            x_turn(1, 1, 0)
+            w_group(1, 0, False)
+            x_out(1, 0, 0, False)
+            x_turn(1, 1, 1)
             x_turn(1, 2, 1)
-            p_scale(0, 6, False)
-            wd_quant(1, 1)
-            g_open(1, 1, 1)
-            g_pass(1, 1, 1, 0)
-            g_pass(0, 2, 1, 3)
+            x_out(1, 1, 1, False)
+            x_turn(1, 2, 0)
+            w_quant(1, 1)
+            x_out(1, 1, 0, False)
+            x_turn(1, 3, 0)
+            w_quant(1, 0)
+            x_out(1, 2, 0, False)
+            x_turn(1, 3, 1)
+            wd_make(1, 3)
+            p_unit(0, 5)
+            x_out(1, 3, 1, False)
+            p_scale(0, 0, False)
+            p_scale(0, 3, True)
+            p_pass(accs[0, 2], 0, 2, 3)
             x_out(1, 2, 1, False)
-            x_quant(1, 0)
-            p_open(0, 5)
-            p_pass(accs[0, 5], 0, 5, 0)
-            g_pass(0, 1, 1, 3)
-            p_keep(0, 7, False)
-            p_pass(accs[0, 5], 0, 5, 1)
+            g_unit(0, 3, 1)
             wd_quant(1, 3)
-            g_pass(1, 1, 1, 1)
-            g_out(0, 2, 1, False)
-            g_open(1, 0, 1)
-            g_pass(1, 0, 1, 0)
-            x_quant(1, 2)
-            g_pass(1, 1, 1, 2)
-            g_out(0, 1, 1, False)
-            g_open(1, 0, 0)
-            g_pass(1, 0, 0, 0)
-            x_quant(1, 3)
-            g_pass(1, 2, 1, 1)
-            g_pass(1, 1, 1, 3)
-            p_keep(0, 6, True)
-            g_pass(1, 2, 1, 2)
-            g_pass(1, 0, 0, 1)
-            g_out(1, 1, 1, True)
-            g_open(1, 3, 1)
-            g_pass(1, 3, 1, 0)
-            p_pass(accs[0, 5], 0, 5, 2)
-            g_open(1, 3, 0)
-            g_pass(1, 3, 0, 0)
-            g_group(0, 0)
-            p_open(1, 6)
-            p_pass(accs[1, 6], 1, 6, 0)
-            g_pass(1, 0, 0, 2)
-            g_pass(1, 3, 1, 1)
-            p_pass(accs[1, 6], 1, 6, 1)
-            g_pass(1, 3, 1, 2)
-            ps_group(0, 0)
-            g_pass(1, 2, 1, 3)
-            p_pass(accs[0, 5], 0, 5, 3)
-            g_open(1, 1, 0)
-            g_pass(1, 1, 0, 0)
-            g_pass(1, 3, 1, 3)
+            x_out(1, 3, 0, False)
+            wd_make(1, 2)
+            g_unit(0, 1, 1)
+            p_keep(0, 3, False)
             p_scale(0, 5, False)
-            g_group(0, 1)
-            g_pass(1, 0, 1, 1)
-            g_pass(1, 0, 0, 3)
+            x_quant(1, 1)
+            p_unit(0, 7)
+            g_out(0, 1, 1, True)
+            wd_make(1, 0)
+            g_unit(0, 2, 1)
+            p_scale(0, 7, False)
+            x_quant(1, 0)
+            p_keep(0, 7, False)
+            g_unit(0, 0, 1)
+            x_quant(1, 2)
             p_keep(0, 5, False)
-            g_pass(1, 0, 1, 2)
-            g_pass(1, 3, 0, 1)
-            g_pass(1, 0, 1, 3)
-            g_out(1, 0, 0, False)
-            g_quant(0, 0)
-            g_pass(1, 1, 0, 1)
-            p_open(1, 4)
-            p_pass(accs[1, 4], 1, 4, 0)
-            g_out(1, 2, 1, False)
-            g_pass(1, 3, 0, 2)
-            ps_group(0, 1)
-            p_open(1, 5)
-            p_pass(accs[1, 5], 1, 5, 0)
-            g_out(1, 0, 1, False)
-            p_pass(accs[1, 6], 1, 6, 2)
-            p_pass(accs[1, 4], 1, 4, 1)
-            g_out(1, 3, 1, False)
-            g_open(1, 2, 0)
-            g_pass(1, 2, 0, 0)
-            h_turn(0, 2, 0)
-            ps_quant(0, 0)
-            g_pass(1, 1, 0, 2)
-            g_group(1, 1)
-            p_pass(accs[1, 6], 1, 6, 3)
-            p_pass(accs[1, 4], 1, 4, 2)
-            g_pass(1, 2, 0, 1)
-            p_pass(accs[1, 5], 1, 5, 1)
-            g_pass(1, 3, 0, 3)
-            p_open(1, 7)
-            p_pass(accs[1, 7], 1, 7, 0)
-            g_quant(1, 1)
-            p_pass(accs[1, 4], 1, 4, 3)
-            g_out(1, 3, 0, False)
-            g_pass(1, 1, 0, 3)
-            h_out(0, 2, 0, True)
-            p_pass(accs[1, 7], 1, 7, 1)
-            p_scale(1, 6, False)
-            g_pass(1, 2, 0, 2)
-            g_quant(0, 1)
-            p_pass(accs[1, 7], 1, 7, 2)
-            p_scale(1, 4, False)
-            g_pass(1, 2, 0, 3)
-            p_pass(accs[1, 5], 1, 5, 2)
-            ps_quant(0, 1)
-            p_open(1, 2)
-            p_pass(accs[1, 2], 1, 2, 0)
-            p_keep(1, 4, False)
-            h_turn(0, 2, 1)
-            g_out(1, 1, 0, True)
-            p_pass(accs[1, 5], 1, 5, 3)
-            g_out(1, 2, 0, False)
-            p_keep(1, 6, True)
-            p_open(1, 3)
-            p_pass(accs[1, 3], 1, 3, 0)
-            p_open(1, 0)
-            p_pass(accs[1, 0], 1, 0, 0)
-            p_scale(1, 5, False)
-            p_pass(accs[1, 7], 1, 7, 3)
-            g_group(1, 0)
-            p_pass(accs[1, 2], 1, 2, 1)
-            p_pass(accs[1, 0], 1, 0, 1)
-            p_scale(1, 7, False)
-            p_pass(accs[1, 3], 1, 3, 1)
-            p_pass(accs[1, 2], 1, 2, 2)
-            h_out(0, 2, 1, False)
-            p_pass(accs[1, 0], 1, 0, 2)
-            ps_group(1, 1)
-            p_pass(accs[1, 2], 1, 2, 3)
-            p_keep(1, 7, False)
-            p_pass(accs[1, 3], 1, 3, 2)
-            r_side(0, 2, 1)
-            p_scale(1, 2, False)
-            g_quant(1, 0)
-            p_pass(accs[1, 0], 1, 0, 3)
-            p_keep(1, 5, False)
-            p_pass(accs[1, 3], 1, 3, 3)
-            p_open(1, 1)
-            p_pass(accs[1, 1], 1, 1, 0)
-            ps_quant(1, 1)
-            r_side(0, 2, 0)
-            p_scale(1, 3, False)
-            r_side_sum(0, 2, 1)
-            p_pass(accs[1, 1], 1, 1, 1)
-            p_keep(1, 3, False)
-            r_side(0, 3, 0)
-            r_side_sum(0, 2, 0)
+            wd_quant(1, 2)
+            p_unit(0, 4)
+            g_out(0, 0, 1, False)
+            x_quant(1, 3)
+            g_out(0, 3, 1, False)
+            p_unit(0, 6)
+            g_out(0, 2, 1, True)
+            p_scale(0, 2, False)
+            wd_quant(1, 0)
+            p_unit(1, 0)
+            p_keep(0, 2, False)
+            wd_make(1, 1)
+            p_unit(1, 7)
+            p_scale(0, 1, True)
             p_scale(1, 0, False)
-            p_pass(accs[1, 1], 1, 1, 2)
-            h_turn(0, 1, 1)
-            r_side_sum(0, 3, 0)
-            p_keep(1, 2, False)
-            p_pass(accs[1, 1], 1, 1, 3)
-            r_side_sort(0, 2)
-            h_turn(0, 0, 0)
+            wd_quant(1, 1)
+            p_scale(0, 6, False)
+            p_unit(1, 1)
+            ps_group(0, 0, False)
+            p_keep(0, 1, False)
+            p_keep(0, 0, False)
+            g_unit(1, 3, 1)
+            p_scale(1, 7, False)
+            g_group(0, 0)
+            g_unit(1, 0, 1)
+            p_keep(0, 6, False)
+            p_scale(0, 4, True)
+            g_unit(1, 1, 1)
+            g_out(1, 0, 1, True)
+            ps_group(0, 1, False)
+            g_unit(1, 0, 0)
+            g_unit(1, 1, 0)
+            g_group(0, 1)
+            g_out(1, 0, 0, False)
+            p_keep(0, 4, False)
+            p_unit(1, 4)
+            g_out(1, 3, 1, False)
+            g_quant(0, 1)
+            g_out(1, 1, 1, False)
+            g_unit(1, 2, 1)
+            g_quant(0, 0)
+            g_out(1, 1, 0, False)
+            ps_quant(0, 1)
+            p_unit(1, 2)
+            g_out(1, 2, 1, False)
             p_scale(1, 1, False)
-            h_turn(0, 3, 1)
-            r_side(0, 3, 1)
-            h_out(0, 3, 1, False)
-            ps_group(1, 0)
-            h_turn(1, 0, 1)
-            h_turn(0, 0, 1)
-            h_out(1, 0, 1, False)
-            r_side(0, 0, 0)
-            r_side_sum(0, 3, 1)
-            h_out(0, 1, 1, False)
-            r_side(0, 1, 1)
-            ps_quant(1, 0)
-            h_out(0, 0, 0, False)
-            h_turn(1, 2, 1)
-            r_side(0, 1, 0)
-            p_keep(1, 1, False)
-            r_side_sort(0, 3)
-            r_side(0, 0, 1)
+            g_group(1, 1)
+            g_unit(1, 3, 0)
+            p_keep(1, 7, False)
             p_keep(1, 0, False)
-            h_turn(0, 1, 0)
-            h_out(0, 0, 1, False)
-            r_side_sum(0, 1, 1)
-            r_unit(1, 3, 0)
-            h_out(0, 1, 0, False)
-            r_side_sum(0, 0, 0)
-            h_turn(1, 0, 0)
-            h_out(1, 2, 1, False)
-            h_turn(1, 3, 0)
-            r_side_sum(0, 0, 1)
-            h_turn(1, 1, 0)
-            r_side_sum(0, 1, 0)
-            h_out(1, 3, 0, False)
-            h_turn(1, 2, 0)
-            h_turn(1, 1, 1)
-            r_side_sort(0, 0)
-            h_turn(1, 3, 1)
-            r_unit(1, 2, 1)
-            h_out(1, 3, 1, False)
-            r_side_sort(0, 1)
-            r_unit(1, 0, 1)
-            h_out(1, 0, 0, False)
+            g_unit(1, 2, 0)
+            p_scale(1, 2, False)
+            g_quant(1, 1)
+            p_unit(1, 3)
+            p_scale(1, 4, False)
+            ps_quant(0, 0)
+            g_out(1, 2, 0, False)
+            g_out(1, 3, 0, True)
+            p_unit(1, 5)
+            p_scale(1, 3, False)
+            g_group(1, 0)
+            ps_group(1, 0, True)
+            p_unit(1, 6)
+            p_scale(1, 5, False)
+            p_keep(1, 3, True)
+            p_keep(1, 1, False)
+            r_unit(0, 1, 1)
+            g_quant(1, 0)
+            p_scale(1, 6, False)
+            r_unit(0, 3, 1)
+            p_keep(1, 2, True)
+            r_copy(0, 1, 1)
+            r_unit(0, 0, 1)
+            ps_group(1, 1, False)
+            p_keep(1, 4, False)
+            r_add(0, 1, 1)
+            r_unit(0, 2, 1)
+            r_copy(0, 0, 1)
+            r_unit(0, 1, 0)
+            ps_quant(1, 0)
+            p_keep(1, 5, False)
+            r_add(0, 0, 1)
+            r_unit(0, 2, 0)
+            ps_quant(1, 1)
+            r_copy(0, 3, 1)
+            r_unit(0, 0, 0)
+            r_copy(0, 2, 1)
+            r_sum(0, 2, 0)
             r_unit(1, 1, 1)
-            h_out(1, 1, 0, False)
+            r_sum(0, 1, 0)
+            r_add(0, 2, 1)
             r_unit(1, 1, 0)
-            r_sum(1, 3, 0)
-            h_out(1, 1, 1, False)
-            r_unit(1, 0, 0)
-            r_sum(1, 0, 1)
-            h_out(1, 2, 0, False)
-            r_unit(1, 3, 1)
+            h_turn(0, 1, 1)
             r_sum(1, 1, 0)
-            o_group(0, 0, 0, False)
-            r_unit(1, 2, 0)
-            r_sum(1, 1, 1)
-            r_sort(1, 0, 1)
-            o_group(0, 0, 1, False)
-            r_sort(1, 1, 1)
-            r_sort(1, 1, 0)
-            o_group(0, 1, 0, False)
-            r_sum(1, 3, 1)
-            r_sum(1, 2, 1)
-            o_group(0, 1, 1, False)
-            r_sort(1, 3, 1)
-            r_sort(1, 2, 1)
+            r_add(0, 3, 1)
+            h_turn(0, 1, 0)
+            h_out(0, 1)
+            h_turn(0, 2, 1)
+            r_sum(0, 0, 0)
+            h_turn(0, 2, 0)
+            h_out(0, 2)
+            h_turn(0, 0, 1)
+            r_pick(0, 1, 0)
+            r_unit(0, 3, 0)
+            r_copy(1, 1, 1)
+            r_pick(0, 2, 0)
+            r_unit(1, 2, 1)
+            p_keep(1, 6, False)
+            r_sum(0, 3, 0)
+            h_turn(0, 0, 0)
+            h_out(0, 0)
+            r_add(1, 1, 1)
+            r_pick(0, 2, 1)
+            h_turn(0, 3, 0)
+            r_copy(1, 2, 1)
+            h_turn(0, 3, 1)
+            r_pick(0, 0, 0)
+            r_unit(1, 3, 1)
+            h_out(0, 3)
+            r_pick(0, 1, 1)
+            r_add(1, 2, 1)
+            r_unit(1, 3, 0)
+            r_pick(0, 3, 0)
+            r_copy(1, 3, 1)
+            r_unit(1, 0, 0)
+            r_pick(0, 0, 1)
+            o_group(0, 0, 1, "s")
+            r_add(1, 3, 1)
+            r_unit(1, 0, 1)
+            r_pick(0, 3, 1)
+            h_turn(1, 1, 1)
+            r_sum(1, 3, 0)
+            o_group(0, 0, 0, "g")
+            h_turn(1, 1, 0)
+            h_out(1, 1)
+            h_turn(1, 3, 1)
             r_sum(1, 0, 0)
-            o_group(1, 1, 0, False)
+            r_unit(1, 2, 0)
+            r_copy(1, 0, 1)
+            r_pick(1, 1, 0)
+            h_turn(1, 3, 0)
+            h_out(1, 3)
+            r_add(1, 0, 1)
             r_sum(1, 2, 0)
-            r_sort(1, 3, 0)
-            o_group(1, 1, 1, False)
-            r_sort(1, 0, 0)
-            r_sort(1, 2, 0)
-            o_quant(0, 1)
-            o_group(1, 0, 1, False)
-            o_group(1, 0, 0, True)
-            o_quant(1, 1)
+            h_turn(1, 2, 1)
+            o_group(0, 1, 1, "s")
+            h_turn(1, 0, 0)
+            r_pick(1, 3, 0)
+            h_turn(1, 2, 0)
             o_quant(0, 0)
+            h_turn(1, 0, 1)
+            h_out(1, 2)
+            r_pick(1, 3, 1)
+            h_out(1, 0)
+            r_pick(1, 2, 0)
+            o_group(0, 1, 0, "s")
+            r_pick(1, 0, 0)
+            r_pick(1, 1, 1)
+            o_group(1, 0, 0, "s")
+            r_pick(1, 2, 1)
+            o_quant(0, 1)
+            o_group(1, 0, 1, "s")
+            r_pick(1, 0, 1)
+            o_group(1, 1, 0, "v")
+            o_group(1, 1, 1, "s")
             o_quant(1, 0)
+            o_quant(1, 1)

@@ -33,20 +33,16 @@ def tile_bjorckmaxmindense_x1_kernel(tc, x, w, d, s, t, b, out, out_words, out_s
 
         d_cols = const.tile([P, NC, 4], BF16)
         nc.scalar.dma_start(out=d_cols[:], in_=d.rearrange("(c p j) -> p c j", p=P, j=4))
-        s_bf = const.tile([P, 2, 4], BF16)
-        t_bf = const.tile([P, 2, 4], BF16)
-        b_bf = const.tile([P, 2, 4], BF16)
-        for tile_, vec in ((s_bf, s), (b_bf, b), (t_bf, t)):
-            nc.scalar.dma_start(out=tile_[:], in_=vec.rearrange("(g p t) -> p g t", p=P, t=4))
         ident = const.tile([P, P], F32)
         make_identity(nc, ident[:])
 
         w_raw, x_raw = {}, {}
 
         def load_w(g, c):
-            w_raw[g, c] = t4.tile([P, 4, W], BF16, name="t4", align_bytes=64)
+            tile_ = t4.tile([P, 4, W], BF16, name="t4", align_bytes=64)
             src = w[c * W : (c + 1) * W, g * W : (g + 1) * W].rearrange("(p j) f -> p j f", j=4)
-            nc.sync.dma_start(out=w_raw[g, c][:], in_=src)
+            nc.sync.dma_start(out=tile_[:], in_=src)
+            w_raw[g, c] = tile_[:]
 
         def load_x(tg, kh):
             x_raw[tg, kh] = t8.tile([P, 4, 1024], BF16, name="t8", align_bytes=64)
@@ -64,12 +60,13 @@ def tile_bjorckmaxmindense_x1_kernel(tc, x, w, d, s, t, b, out, out_words, out_s
         load_x(1, 0)
         load_x(1, 1)
 
-        s_cols = const.tile([P, 2, 4], F32)
-        nc.vector.tensor_copy(out=s_cols[:], in_=s_bf[:])
-        t_cols = const.tile([P, 2, 4], F32)
-        nc.vector.tensor_copy(out=t_cols[:], in_=t_bf[:])
-        b_cols = const.tile([P, 2, 4], F32)
-        nc.vector.tensor_copy(out=b_cols[:], in_=b_bf[:])
+        cols = {}
+        for name, vec in (("s", s), ("b", b), ("t", t)):
+            rows = const.tile([P, 2, 4], BF16, name=name + "_bf16")
+            nc.sync.dma_start(out=rows[:], in_=vec.rearrange("(g p t) -> p g t", p=P, t=4))
+            cols[name] = const.tile([P, 2, 4], F32, name=name + "_cols")
+            nc.gpsimd.tensor_copy(out=cols[name][:], in_=rows[:])
+        s_cols, b_cols, t_cols = cols["s"], cols["b"], cols["t"]
 
         def codes(name, width):
             return (
@@ -104,8 +101,8 @@ def tile_bjorckmaxmindense_x1_kernel(tc, x, w, d, s, t, b, out, out_words, out_s
 
         def w_group(g, c, on_scalar):
             wg[g, c] = t4.tile([P, 4 * W], BF16, name="t4", align_bytes=64)
-            dst = wg[g, c][:].rearrange("p (t m j) -> p t m j", t=4, j=4)
-            src = w_raw[g, c][:].rearrange("p j (m t) -> p t m j", t=4)
+            dst = wg[g, c][:].rearrange("p (t m j) -> p m j t", t=4, j=4)
+            src = w_raw[g, c].rearrange("p j (m t) -> p m j t", t=4)
             if on_scalar:
                 nc.scalar.copy(out=dst, in_=src)
             else:
@@ -189,13 +186,15 @@ def tile_bjorckmaxmindense_x1_kernel(tc, x, w, d, s, t, b, out, out_words, out_s
 
         def ps_group(tg, g, on_gpsimd=False):
             psg[tg, g] = t4.tile([P, W, 4], BF16, name="t4", align_bytes=64)
-            src = psraw[tg, g][:].rearrange("p t n -> p n t")
+            dst, src = psg[tg, g][:], psraw[tg, g][:]
             if on_gpsimd:
                 nc.gpsimd.tensor_scalar(
-                    out=psg[tg, g][:], in0=src, scalar1=1.0, scalar2=0.0, op0=ALU.mult, op1=ALU.add
+                    out=dst, in0=src.rearrange("p t n -> p n t"), scalar1=1.0, scalar2=0.0, op0=ALU.mult, op1=ALU.add
                 )
             else:
-                nc.vector.tensor_copy(out=psg[tg, g][:], in_=src)
+                nc.vector.tensor_copy(
+                    out=dst.rearrange("p (c i) t -> p c t i", i=4), in_=src.rearrange("p t (c i) -> p c t i", i=4)
+                )
 
         def ps_quant(tg, g):
             quantize(psq[tg, g], 0, W, psg[tg, g][:].rearrange("p n t -> p (n t)"))
@@ -225,7 +224,10 @@ def tile_bjorckmaxmindense_x1_kernel(tc, x, w, d, s, t, b, out, out_words, out_s
 
         def g_group(gi, jg):
             gg[gi, jg] = t4.tile([P, W, 4], BF16, name="t4", align_bytes=64)
-            nc.vector.tensor_copy(out=gg[gi, jg][:], in_=graw[gi, jg][:].rearrange("p t n -> p n t"))
+            nc.vector.tensor_copy(
+                out=gg[gi, jg][:].rearrange("p (c i) t -> p c t i", i=4),
+                in_=graw[gi, jg][:].rearrange("p t (c i) -> p c t i", i=4),
+            )
 
         def g_quant(gi, jg):
             quantize(gq[gi, jg], 0, W, gg[gi, jg][:].rearrange("p n t -> p (n t)"))
@@ -289,16 +291,18 @@ def tile_bjorckmaxmindense_x1_kernel(tc, x, w, d, s, t, b, out, out_words, out_s
             if (tg, side) not in ob:
                 ob[tg, side] = t4.tile([P, W, 4], BF16, name="t4", align_bytes=64)
             cols = slice(half * 256, half * 256 + 256)
-            dst = ob[tg, side][:, cols, :]
-            src = outs[tg, side][:, :, cols].rearrange("p t f -> p f t")
-            if eng == "v":
-                nc.vector.tensor_copy(out=dst, in_=src)
-            elif eng == "s":
-                nc.scalar.copy(out=dst, in_=src)
-            else:
+            dst, src = ob[tg, side][:, cols, :], outs[tg, side][:, :, cols]
+            if eng == "g":
                 nc.gpsimd.tensor_scalar(
-                    out=dst, in0=src, scalar1=1.0, scalar2=0.0, op0=ALU.mult, op1=ALU.add
+                    out=dst, in0=src.rearrange("p t f -> p f t"), scalar1=1.0, scalar2=0.0, op0=ALU.mult, op1=ALU.add
                 )
+            else:
+                dst = dst.rearrange("p (c i) t -> p c t i", i=4)
+                src = src.rearrange("p t (c i) -> p c t i", i=4)
+                if eng == "v":
+                    nc.vector.tensor_copy(out=dst, in_=src)
+                else:
+                    nc.scalar.copy(out=dst, in_=src)
 
         def o_quant(tg, side):
             oq = oqp.tile([P, W], U32, name="oq", align_bytes=64)

@@ -25,9 +25,9 @@ def tile_bjorckmaxmindense_x1_kernel(tc, x, w, d, s, t, b, out, out_words, out_s
     with ExitStack() as ctx:
         const = ctx.enter_context(tc.tile_pool(name="const", bufs=1))
         t8 = ctx.enter_context(tc.tile_pool(name="t8", bufs=7))
-        t4 = ctx.enter_context(tc.tile_pool(name="t4", bufs=18))
+        t4 = ctx.enter_context(tc.tile_pool(name="t4", bufs=17))
         keep = ctx.enter_context(tc.tile_pool(name="keep", bufs=1))
-        hp = ctx.enter_context(tc.tile_pool(name="hp", bufs=3))
+        hp = ctx.enter_context(tc.tile_pool(name="hp", bufs=4))
         oqp = ctx.enter_context(tc.tile_pool(name="oqp", bufs=4))
         ps = ctx.enter_context(tc.psum_pool(name="ps", bufs=8))
 
@@ -49,24 +49,28 @@ def tile_bjorckmaxmindense_x1_kernel(tc, x, w, d, s, t, b, out, out_words, out_s
             src = x[tg * W : (tg + 1) * W, kh * 1024 : (kh + 1) * 1024].rearrange("(m t) k -> m t k", t=4)
             nc.sync.dma_start(out=x_raw[tg, kh][:], in_=src)
 
+        cols = {}
+
+        def load_vectors():
+            for name, vec in (("s", s), ("b", b), ("t", t)):
+                rows = const.tile([P, 2, 4], BF16, name=name + "_bf16")
+                nc.sync.dma_start(out=rows[:], in_=vec.rearrange("(g p t) -> p g t", p=P, t=4))
+                cols[name] = const.tile([P, 2, 4], F32, name=name + "_cols")
+                nc.gpsimd.tensor_copy(out=cols[name][:], in_=rows[:])
+
         load_w(0, 0)
         load_w(0, 1)
         load_x(0, 0)
         load_w(0, 2)
         load_w(0, 3)
         load_x(0, 1)
+        load_vectors()
         for c in range(NC):
             load_w(1, c)
         load_x(1, 0)
         load_x(1, 1)
-
-        cols = {}
-        for name, vec in (("s", s), ("b", b), ("t", t)):
-            rows = const.tile([P, 2, 4], BF16, name=name + "_bf16")
-            nc.sync.dma_start(out=rows[:], in_=vec.rearrange("(g p t) -> p g t", p=P, t=4))
-            cols[name] = const.tile([P, 2, 4], F32, name=name + "_cols")
-            nc.gpsimd.tensor_copy(out=cols[name][:], in_=rows[:])
         s_cols, b_cols, t_cols = cols["s"], cols["b"], cols["t"]
+
 
         def codes(name, width):
             return (
@@ -323,288 +327,287 @@ def tile_bjorckmaxmindense_x1_kernel(tc, x, w, d, s, t, b, out, out_words, out_s
             wd_quant(0, 0)
             x_turn(0, 0, 0)
             wd_make(0, 1)
-            x_turn(0, 0, 1)
-            x_out(0, 0, 0, False)
-            g_open(0, 1, 0)
-            g_pass(0, 1, 0, 0)
-            w_quant(0, 1)
-            x_out(0, 0, 1, False)
-            g_open(0, 3, 0)
-            g_pass(0, 3, 0, 0)
-            g_open(0, 0, 0)
-            g_pass(0, 0, 0, 0)
-            w_group(0, 2, True)
-            wd_quant(0, 1)
-            x_turn(0, 1, 0)
-            x_quant(0, 0)
             g_open(0, 2, 0)
             g_pass(0, 2, 0, 0)
-            g_pass(0, 1, 0, 1)
-            w_group(0, 3, False)
-            p_open(0, 1)
-            p_pass(accs[0, 1], 0, 1, 0)
-            g_pass(0, 0, 0, 1)
-            g_pass(0, 2, 0, 1)
-            g_pass(0, 3, 0, 1)
+            w_group(0, 2, True)
+            w_quant(0, 1)
+            g_open(0, 3, 0)
+            g_pass(0, 3, 0, 0)
+            wd_quant(0, 1)
+            x_turn(0, 0, 1)
+            x_out(0, 0, 0, True)
+            x_turn(0, 1, 0)
+            x_out(0, 0, 1, True)
+            g_open(0, 0, 0)
+            g_pass(0, 0, 0, 0)
             x_out(0, 1, 0, False)
-            x_turn(0, 1, 1)
+            g_pass(0, 3, 0, 1)
             wd_make(0, 2)
-            x_turn(0, 3, 0)
-            x_out(0, 1, 1, False)
-            x_turn(0, 3, 1)
+            g_pass(0, 2, 0, 1)
+            w_group(0, 3, True)
+            g_pass(0, 0, 0, 1)
+            x_turn(0, 1, 1)
             w_quant(0, 2)
-            x_out(0, 3, 0, False)
             x_turn(0, 2, 0)
             wd_quant(0, 2)
+            x_turn(0, 3, 1)
+            x_quant(0, 0)
+            g_open(0, 1, 0)
+            g_pass(0, 1, 0, 0)
+            g_pass(0, 1, 0, 1)
+            x_out(0, 1, 1, False)
+            wd_make(0, 3)
+            x_turn(0, 3, 0)
             x_out(0, 3, 1, False)
             x_turn(0, 2, 1)
+            x_out(0, 3, 0, False)
             x_quant(0, 1)
-            x_out(0, 2, 0, False)
-            p_open(0, 2)
-            p_pass(accs[0, 2], 0, 2, 0)
-            wd_make(0, 3)
-            g_pass(0, 3, 0, 2)
-            x_out(0, 2, 1, False)
-            p_open(0, 3)
-            p_pass(accs[0, 3], 0, 3, 0)
-            g_pass(0, 2, 0, 2)
-            w_group(1, 1, True)
             g_pass(0, 1, 0, 2)
-            x_quant(0, 2)
-            p_pass(accs[0, 3], 0, 3, 1)
-            p_pass(accs[0, 1], 0, 1, 1)
+            x_out(0, 2, 1, False)
+            g_pass(0, 2, 0, 2)
+            x_out(0, 2, 0, True)
             p_open(0, 0)
             p_pass(accs[0, 0], 0, 0, 0)
+            w_group(1, 1, True)
+            p_open(0, 2)
+            p_pass(accs[0, 2], 0, 2, 0)
             wd_quant(0, 3)
-            p_pass(accs[0, 0], 0, 0, 1)
-            p_pass(accs[0, 1], 0, 1, 2)
+            p_open(0, 3)
+            p_pass(accs[0, 3], 0, 3, 0)
+            p_pass(accs[0, 3], 0, 3, 1)
             w_quant(0, 3)
-            p_pass(accs[0, 3], 0, 3, 2)
-            g_pass(0, 0, 0, 2)
-            x_quant(0, 3)
-            p_pass(accs[0, 0], 0, 0, 2)
-            w_group(1, 3, True)
+            g_pass(0, 3, 0, 2)
             p_pass(accs[0, 2], 0, 2, 1)
-            w_group(1, 2, False)
-            g_pass(0, 2, 0, 3)
-            p_pass(accs[0, 1], 0, 1, 3)
-            g_pass(0, 3, 0, 3)
-            g_pass(0, 1, 0, 3)
-            p_pass(accs[0, 0], 0, 0, 3)
-            g_out(0, 2, 0, True)
+            x_quant(0, 2)
+            g_pass(0, 0, 0, 2)
+            p_open(0, 1)
+            p_pass(accs[0, 1], 0, 1, 0)
+            x_quant(0, 3)
             g_pass(0, 0, 0, 3)
-            p_pass(accs[0, 3], 0, 3, 3)
-            g_out(0, 1, 0, True)
-            p_pass(accs[0, 2], 0, 2, 2)
-            g_out(0, 3, 0, False)
-            x_turn(1, 0, 1)
-            w_quant(1, 3)
+            p_pass(accs[0, 1], 0, 1, 1)
+            w_group(1, 2, False)
+            g_pass(0, 3, 0, 3)
             g_out(0, 0, 0, False)
-            x_turn(1, 0, 0)
-            w_quant(1, 2)
-            x_out(1, 0, 1, False)
-            x_turn(1, 1, 0)
-            w_group(1, 0, False)
-            x_out(1, 0, 0, False)
-            x_turn(1, 1, 1)
-            x_turn(1, 2, 1)
-            x_out(1, 1, 1, False)
-            x_turn(1, 2, 0)
+            g_pass(0, 2, 0, 3)
+            p_pass(accs[0, 0], 0, 0, 1)
+            w_group(1, 3, True)
+            p_pass(accs[0, 1], 0, 1, 2)
+            g_pass(0, 1, 0, 3)
             w_quant(1, 1)
-            x_out(1, 1, 0, False)
-            x_turn(1, 3, 0)
-            w_quant(1, 0)
-            x_out(1, 2, 0, False)
-            x_turn(1, 3, 1)
-            wd_make(1, 3)
-            p_unit(0, 5)
-            x_out(1, 3, 1, False)
-            p_scale(0, 0, False)
-            p_scale(0, 3, True)
+            p_pass(accs[0, 2], 0, 2, 2)
+            p_pass(accs[0, 1], 0, 1, 3)
+            g_out(0, 1, 0, True)
             p_pass(accs[0, 2], 0, 2, 3)
-            x_out(1, 2, 1, False)
-            g_unit(0, 3, 1)
-            wd_quant(1, 3)
-            x_out(1, 3, 0, False)
+            p_pass(accs[0, 3], 0, 3, 2)
+            w_group(1, 0, False)
+            x_turn(1, 1, 0)
+            x_turn(1, 0, 0)
+            x_out(1, 1, 0, False)
+            p_pass(accs[0, 0], 0, 0, 2)
+            w_quant(1, 3)
+            g_out(0, 2, 0, False)
+            p_pass(accs[0, 0], 0, 0, 3)
+            x_turn(1, 2, 0)
+            w_quant(1, 0)
+            g_out(0, 3, 0, False)
+            w_quant(1, 2)
+            x_turn(1, 2, 1)
+            x_out(1, 2, 0, False)
+            x_turn(1, 1, 1)
             wd_make(1, 2)
-            g_unit(0, 1, 1)
-            p_keep(0, 3, False)
-            p_scale(0, 5, False)
+            p_scale(0, 0, False)
+            p_pass(accs[0, 3], 0, 3, 3)
+            g_unit(0, 3, 1)
+            x_out(1, 1, 1, False)
+            x_out(1, 0, 0, False)
             x_quant(1, 1)
-            p_unit(0, 7)
-            g_out(0, 1, 1, True)
+            g_unit(0, 0, 1)
+            p_scale(0, 3, False)
+            wd_make(1, 3)
+            p_scale(0, 1, False)
+            g_unit(0, 1, 1)
+            x_out(1, 2, 1, False)
+            wd_quant(1, 2)
+            p_keep(0, 3, False)
+            wd_quant(1, 3)
+            p_unit(0, 6)
+            g_out(0, 3, 1, False)
+            p_keep(0, 1, True)
+            g_out(0, 0, 1, False)
             wd_make(1, 0)
             g_unit(0, 2, 1)
-            p_scale(0, 7, False)
-            x_quant(1, 0)
-            p_keep(0, 7, False)
-            g_unit(0, 0, 1)
-            x_quant(1, 2)
-            p_keep(0, 5, False)
-            wd_quant(1, 2)
-            p_unit(0, 4)
-            g_out(0, 0, 1, False)
-            x_quant(1, 3)
-            g_out(0, 3, 1, False)
-            p_unit(0, 6)
-            g_out(0, 2, 1, True)
-            p_scale(0, 2, False)
-            wd_quant(1, 0)
-            p_unit(1, 0)
-            p_keep(0, 2, False)
-            wd_make(1, 1)
-            p_unit(1, 7)
-            p_scale(0, 1, True)
-            p_scale(1, 0, False)
-            wd_quant(1, 1)
             p_scale(0, 6, False)
-            p_unit(1, 1)
-            ps_group(0, 0, False)
-            p_keep(0, 1, False)
-            p_keep(0, 0, False)
-            g_unit(1, 3, 1)
-            p_scale(1, 7, False)
+            wd_make(1, 1)
+            x_turn(1, 0, 1)
+            g_out(0, 2, 1, False)
+            x_turn(1, 3, 0)
+            x_quant(1, 2)
+            x_turn(1, 3, 1)
+            wd_quant(1, 0)
+            p_unit(0, 7)
+            x_out(1, 3, 1, False)
+            wd_quant(1, 1)
+            p_scale(0, 2, False)
+            x_out(1, 3, 0, True)
+            p_unit(0, 5)
+            x_out(1, 0, 1, False)
             g_group(0, 0)
+            g_out(0, 1, 1, False)
             g_unit(1, 0, 1)
-            p_keep(0, 6, False)
-            p_scale(0, 4, True)
-            g_unit(1, 1, 1)
-            g_out(1, 0, 1, True)
-            ps_group(0, 1, False)
-            g_unit(1, 0, 0)
-            g_unit(1, 1, 0)
+            p_scale(0, 5, False)
             g_group(0, 1)
-            g_out(1, 0, 0, False)
-            p_keep(0, 4, False)
-            p_unit(1, 4)
-            g_out(1, 3, 1, False)
-            g_quant(0, 1)
-            g_out(1, 1, 1, False)
-            g_unit(1, 2, 1)
-            g_quant(0, 0)
-            g_out(1, 1, 0, False)
-            ps_quant(0, 1)
-            p_unit(1, 2)
-            g_out(1, 2, 1, False)
-            p_scale(1, 1, False)
-            g_group(1, 1)
+            p_keep(0, 0, False)
+            g_unit(1, 1, 1)
+            g_out(1, 0, 1, False)
+            p_scale(0, 7, True)
             g_unit(1, 3, 0)
-            p_keep(1, 7, False)
-            p_keep(1, 0, False)
-            g_unit(1, 2, 0)
-            p_scale(1, 2, False)
-            g_quant(1, 1)
-            p_unit(1, 3)
-            p_scale(1, 4, False)
+            x_quant(1, 3)
+            p_keep(0, 7, False)
+            g_out(1, 1, 1, True)
+            p_unit(0, 4)
+            x_quant(1, 0)
+            ps_group(0, 0, False)
+            g_unit(1, 3, 1)
+            p_keep(0, 6, True)
+            g_unit(1, 2, 1)
+            g_out(1, 3, 1, False)
+            g_quant(0, 0)
             ps_quant(0, 0)
+            p_unit(1, 3)
+            g_out(1, 2, 1, False)
+            p_keep(0, 5, False)
+            p_unit(1, 2)
+            g_group(1, 1)
+            p_keep(0, 2, False)
+            p_scale(0, 4, False)
+            g_unit(1, 1, 0)
+            ps_group(0, 1, False)
+            p_unit(1, 1)
+            g_out(1, 1, 0, False)
+            p_scale(1, 3, True)
+            p_scale(1, 2, False)
+            p_unit(1, 0)
+            p_scale(1, 1, True)
+            g_quant(0, 1)
+            p_unit(1, 4)
+            p_scale(1, 0, False)
+            p_keep(1, 1, True)
+            p_keep(0, 4, False)
+            ps_quant(0, 1)
+            g_unit(1, 2, 0)
+            p_scale(1, 4, False)
+            g_quant(1, 1)
+            ps_group(1, 0, False)
+            p_unit(1, 7)
             g_out(1, 2, 0, False)
+            p_keep(1, 2, False)
+            g_unit(1, 0, 0)
             g_out(1, 3, 0, True)
+            p_keep(1, 0, False)
+            ps_quant(1, 0)
             p_unit(1, 5)
-            p_scale(1, 3, False)
-            g_group(1, 0)
-            ps_group(1, 0, True)
+            g_out(1, 0, 0, False)
+            p_scale(1, 7, False)
             p_unit(1, 6)
+            g_group(1, 0)
             p_scale(1, 5, False)
-            p_keep(1, 3, True)
-            p_keep(1, 1, False)
-            r_unit(0, 1, 1)
+            r_unit(0, 3, 1)
+            p_keep(1, 5, False)
+            r_unit(0, 0, 1)
             g_quant(1, 0)
             p_scale(1, 6, False)
-            r_unit(0, 3, 1)
-            p_keep(1, 2, True)
-            r_copy(0, 1, 1)
-            r_unit(0, 0, 1)
-            ps_group(1, 1, False)
-            p_keep(1, 4, False)
-            r_add(0, 1, 1)
             r_unit(0, 2, 1)
-            r_copy(0, 0, 1)
+            r_copy(0, 3, 1)
+            ps_group(1, 1, False)
+            p_keep(1, 6, False)
             r_unit(0, 1, 0)
-            ps_quant(1, 0)
-            p_keep(1, 5, False)
-            r_add(0, 0, 1)
+            r_add(0, 3, 1)
+            r_copy(0, 2, 1)
+            r_unit(0, 1, 1)
+            r_copy(0, 0, 1)
             r_unit(0, 2, 0)
             ps_quant(1, 1)
-            r_copy(0, 3, 1)
+            r_add(0, 2, 1)
+            r_copy(0, 1, 1)
+            r_unit(0, 3, 0)
+            p_keep(1, 4, True)
+            p_keep(1, 7, False)
+            r_sum(0, 1, 0)
             r_unit(0, 0, 0)
-            r_copy(0, 2, 1)
+            r_add(0, 1, 1)
             r_sum(0, 2, 0)
             r_unit(1, 1, 1)
-            r_sum(0, 1, 0)
-            r_add(0, 2, 1)
-            r_unit(1, 1, 0)
-            h_turn(0, 1, 1)
-            r_sum(1, 1, 0)
-            r_add(0, 3, 1)
-            h_turn(0, 1, 0)
-            h_out(0, 1)
+            r_sum(0, 3, 0)
+            r_unit(1, 3, 1)
+            r_add(0, 0, 1)
             h_turn(0, 2, 1)
+            r_sum(1, 3, 1)
+            h_turn(0, 1, 0)
+            h_turn(0, 1, 1)
+            h_out(0, 2)
             r_sum(0, 0, 0)
             h_turn(0, 2, 0)
-            h_out(0, 2)
-            h_turn(0, 0, 1)
-            r_pick(0, 1, 0)
-            r_unit(0, 3, 0)
-            r_copy(1, 1, 1)
-            r_pick(0, 2, 0)
-            r_unit(1, 2, 1)
-            p_keep(1, 6, False)
-            r_sum(0, 3, 0)
-            h_turn(0, 0, 0)
-            h_out(0, 0)
-            r_add(1, 1, 1)
-            r_pick(0, 2, 1)
-            h_turn(0, 3, 0)
-            r_copy(1, 2, 1)
             h_turn(0, 3, 1)
-            r_pick(0, 0, 0)
-            r_unit(1, 3, 1)
-            h_out(0, 3)
-            r_pick(0, 1, 1)
-            r_add(1, 2, 1)
-            r_unit(1, 3, 0)
-            r_pick(0, 3, 0)
-            r_copy(1, 3, 1)
-            r_unit(1, 0, 0)
-            r_pick(0, 0, 1)
-            o_group(0, 0, 1, "s")
-            r_add(1, 3, 1)
+            h_out(0, 1)
             r_unit(1, 0, 1)
-            r_pick(0, 3, 1)
-            h_turn(1, 1, 1)
-            r_sum(1, 3, 0)
-            o_group(0, 0, 0, "g")
-            h_turn(1, 1, 0)
-            h_out(1, 1)
-            h_turn(1, 3, 1)
-            r_sum(1, 0, 0)
-            r_unit(1, 2, 0)
+            r_pick(0, 2, 0)
+            p_keep(1, 3, False)
+            r_pick(0, 1, 0)
+            r_unit(1, 0, 0)
+            r_copy(1, 1, 1)
+            r_pick(0, 2, 1)
+            r_unit(1, 1, 0)
             r_copy(1, 0, 1)
+            r_add(1, 1, 1)
+            r_sum(1, 0, 0)
+            h_out(0, 3)
+            h_turn(0, 0, 1)
+            r_sum(1, 1, 0)
+            h_turn(0, 0, 0)
+            r_unit(1, 2, 1)
+            h_out(0, 0)
+            r_add(1, 0, 1)
+            r_pick(0, 1, 1)
+            h_turn(0, 3, 0)
+            r_pick(0, 0, 0)
+            r_copy(1, 2, 1)
+            h_turn(1, 1, 1)
+            r_unit(1, 2, 0)
+            r_pick(0, 3, 0)
+            r_add(1, 2, 1)
+            r_pick(0, 0, 1)
+            r_unit(1, 3, 0)
+            o_group(0, 0, 0, "s")
+            r_pick(0, 3, 1)
+            h_turn(1, 0, 1)
+            o_group(0, 0, 1, "g")
+            r_sum(1, 2, 0)
+            h_turn(1, 3, 1)
+            h_out(1, 1)
+            h_turn(1, 1, 0)
+            r_sum(1, 3, 0)
+            h_turn(1, 2, 1)
+            h_out(1, 0)
+            h_turn(1, 0, 0)
             r_pick(1, 1, 0)
+            o_group(0, 1, 0, "g")
+            h_turn(1, 2, 0)
+            h_out(1, 2)
+            o_quant(0, 0)
             h_turn(1, 3, 0)
             h_out(1, 3)
-            r_add(1, 0, 1)
-            r_sum(1, 2, 0)
-            h_turn(1, 2, 1)
-            o_group(0, 1, 1, "s")
-            h_turn(1, 0, 0)
-            r_pick(1, 3, 0)
-            h_turn(1, 2, 0)
-            o_quant(0, 0)
-            h_turn(1, 0, 1)
-            h_out(1, 2)
-            r_pick(1, 3, 1)
-            h_out(1, 0)
             r_pick(1, 2, 0)
-            o_group(0, 1, 0, "s")
+            o_group(0, 1, 1, "s")
             r_pick(1, 0, 0)
+            r_pick(1, 3, 0)
             r_pick(1, 1, 1)
             o_group(1, 0, 0, "s")
-            r_pick(1, 2, 1)
+            r_pick(1, 3, 1)
             o_quant(0, 1)
             o_group(1, 0, 1, "s")
+            r_pick(1, 2, 1)
             r_pick(1, 0, 1)
-            o_group(1, 1, 0, "v")
-            o_group(1, 1, 1, "s")
             o_quant(1, 0)
+            o_group(1, 1, 1, "v")
+            o_group(1, 1, 0, "v")
             o_quant(1, 1)

from contextlib import ExitStack

import concourse.mybir as mybir
from concourse.masks import make_identity

N, D, F = 1024, 2048, 1024
FLOPS = 2 * N * F * (D + D + F)

F32 = mybir.dt.float32
BF16 = mybir.dt.bfloat16
U32 = mybir.dt.uint32
I32 = mybir.dt.int32
U8 = mybir.dt.uint8
FP8X4 = mybir.dt.float8_e4m3fn_x4
ALU = mybir.AluOpType
ACT = mybir.ActivationFunctionType

P = 128
W = 512
NC = D // W


def tile_bjorckmaxmindense_x1_kernel(tc, x, w, d, s, t, b, out, out_words, out_scales):
    nc = tc.nc
    with ExitStack() as ctx:
        const = ctx.enter_context(tc.tile_pool(name="const", bufs=1))
        t8 = ctx.enter_context(tc.tile_pool(name="t8", bufs=7))
        t4 = ctx.enter_context(tc.tile_pool(name="t4", bufs=17))
        keep = ctx.enter_context(tc.tile_pool(name="keep", bufs=1))
        hp = ctx.enter_context(tc.tile_pool(name="hp", bufs=4))
        oqp = ctx.enter_context(tc.tile_pool(name="oqp", bufs=4))
        ps = ctx.enter_context(tc.psum_pool(name="ps", bufs=8))

        d_cols = const.tile([P, NC, 4], BF16)
        nc.scalar.dma_start(out=d_cols[:], in_=d.rearrange("(c p j) -> p c j", p=P, j=4))
        ident = const.tile([P, P], F32)
        make_identity(nc, ident[:])

        w_raw, x_raw = {}, {}

        def load_w(g, c):
            tile_ = t4.tile([P, 4, W], BF16, name="t4", align_bytes=64)
            src = w[c * W : (c + 1) * W, g * W : (g + 1) * W].rearrange("(p j) f -> p j f", j=4)
            nc.sync.dma_start(out=tile_[:], in_=src)
            w_raw[g, c] = tile_[:]

        def load_x(tg, kh):
            x_raw[tg, kh] = t8.tile([P, 4, 1024], BF16, name="t8", align_bytes=64)
            src = x[tg * W : (tg + 1) * W, kh * 1024 : (kh + 1) * 1024].rearrange("(m t) k -> m t k", t=4)
            nc.sync.dma_start(out=x_raw[tg, kh][:], in_=src)

        cols = {}

        def load_vectors():
            for name, vec in (("s", s), ("b", b), ("t", t)):
                rows = const.tile([P, 2, 4], BF16, name=name + "_bf16")
                nc.sync.dma_start(out=rows[:], in_=vec.rearrange("(g p t) -> p g t", p=P, t=4))
                cols[name] = const.tile([P, 2, 4], F32, name=name + "_cols")
                nc.gpsimd.tensor_copy(out=cols[name][:], in_=rows[:])

        load_w(0, 0)
        load_w(0, 1)
        load_x(0, 0)
        load_w(0, 2)
        load_w(0, 3)
        load_x(0, 1)
        load_vectors()
        for c in range(NC):
            load_w(1, c)
        load_x(1, 0)
        load_x(1, 1)
        s_cols, b_cols, t_cols = cols["s"], cols["b"], cols["t"]


        def codes(name, width):
            return (
                keep.tile([P, width], U32, name=name + "_q", align_bytes=64),
                keep.tile([P, width], U8, name=name + "_s", align_bytes=64),
            )

        def quantize(dst, lo, width, src):
            nc.vector.quantize_mx(
                out=dst[0][:, lo : lo + width].bitcast(FP8X4),
                scales=dst[1][:, lo : lo + width],
                in_=src,
            )

        def mx(acc, lhs, l0, rhs, r0, n, start, stop):
            nc.tensor.matmul_mx(
                out=acc,
                lhsT=lhs[0][:, l0 : l0 + P].bitcast(FP8X4),
                lhsT_scale=lhs[1][:, l0 : l0 + P],
                rhs=rhs[0][:, r0 : r0 + n].bitcast(FP8X4),
                rhs_scale=rhs[1][:, r0 : r0 + n],
                start=start,
                stop=stop,
            )

        wq = {(g, c): codes("w%d%d" % (g, c), W) for g in range(2) for c in range(NC)}
        wdq = {(g, c): codes("wd%d%d" % (g, c), W) for g in range(2) for c in range(NC)}
        xq = {(tg, c): codes("x%d%d" % (tg, c), W) for tg in range(2) for c in range(NC)}
        gq = {(gi, jg): codes("g%d%d" % (gi, jg), W) for gi in range(2) for jg in range(2)}
        psq = {(tg, gi): codes("ps%d%d" % (tg, gi), W) for tg in range(2) for gi in range(2)}
        wg, wdg = {}, {}

        def w_group(g, c, on_scalar):
            wg[g, c] = t4.tile([P, 4 * W], BF16, name="t4", align_bytes=64)
            dst = wg[g, c][:].rearrange("p (t m j) -> p m j t", t=4, j=4)
            src = w_raw[g, c].rearrange("p j (m t) -> p m j t", t=4)
            if on_scalar:
                nc.scalar.copy(out=dst, in_=src)
            else:
                nc.vector.tensor_copy(out=dst, in_=src)

        def w_quant(g, c):
            quantize(wq[g, c], 0, W, wg[g, c][:])

        def wd_make(g, c):
            wdg[g, c] = t4.tile([P, 4 * W], BF16, name="t4", align_bytes=64)
            nc.vector.tensor_tensor(
                out=wdg[g, c][:].rearrange("p (f j) -> p f j", j=4),
                in0=wg[g, c][:].rearrange("p (f j) -> p f j", j=4),
                in1=d_cols[:, c, :].unsqueeze(1).to_broadcast([P, W, 4]),
                op=ALU.mult,
            )

        def wd_quant(g, c):
            quantize(wdq[g, c], 0, W, wdg[g, c][:])

        xg, xbank = {}, {}

        def x_turn(tg, c, half):
            words = x_raw[tg, c // 2][:].bitcast(F32)
            k0 = 256 * (c % 2)
            bank = ps.tile([P, 2, 2, P], F32, name="bank")
            xbank[tg, c, half] = bank
            for i in range(2):
                for u in range(2):
                    nc.tensor.transpose(bank[:, i, u, :], words[:, 2 * half + i, k0 + u : k0 + 256 : 2], ident[:])

        def x_out(tg, c, half, on_vector=False):
            if (tg, c) not in xg:
                xg[tg, c] = t4.tile([P, W, 2], F32, name="t4", align_bytes=64)
            dst = xg[tg, c][:, half * 256 : (half + 1) * 256, :].rearrange("p (i r) u -> p i r u", i=2)
            src = xbank[tg, c, half][:].rearrange("p i u r -> p i r u")
            if on_vector:
                nc.vector.tensor_copy(out=dst, in_=src)
            else:
                nc.scalar.copy(out=dst, in_=src)

        def x_quant(tg, c):
            quantize(xq[tg, c], 0, W, xg[tg, c][:].rearrange("p r u -> p (r u)").bitcast(BF16))

        h0t = {}
        psraw = {}

        def p_pass(acc, tg, slot, c):
            mx(acc[:], wq[slot // 4, c], slot % 4 * P, xq[tg, c], 0, W, c == 0, c == NC - 1)

        accs, psg = {}, {}

        def p_open(tg, slot):
            accs[tg, slot] = ps.tile([P, W], F32, name="bank")

        def p_unit(tg, slot):
            p_open(tg, slot)
            for c in range(NC):
                p_pass(accs[tg, slot], tg, slot, c)

        def p_scale(tg, slot, on_vector=False):
            g, k = divmod(slot, 4)
            if (tg, g) not in psraw:
                psraw[tg, g] = t4.tile([P, 4, W], BF16, name="t4", align_bytes=64)
            dst, col = psraw[tg, g][:, k, :], s_cols[:, g, k : k + 1]
            if on_vector:
                nc.vector.tensor_scalar(out=dst, in0=accs[tg, slot][:], scalar1=col, scalar2=None, op0=ALU.mult)
            else:
                nc.scalar.activation(out=dst, in_=accs[tg, slot][:], func=ACT.Copy, scale=col)

        def p_keep(tg, slot, on_vector=False):
            g, k = divmod(slot, 4)
            if (tg, g) not in h0t:
                h0t[tg, g] = t8.tile([P, 4, 4, P], F32, name="t8", align_bytes=64)
            dst, col = h0t[tg, g][:, :, k, :], b_cols[:, g, k : k + 1]
            src = accs[tg, slot][:].rearrange("p (q n) -> p q n", q=4)
            if on_vector:
                nc.vector.tensor_scalar(out=dst, in0=src, scalar1=1.5, scalar2=col, op0=ALU.mult, op1=ALU.add)
            else:
                nc.scalar.activation(out=dst, in_=src, func=ACT.Identity, scale=1.5, bias=col)

        def ps_group(tg, g, on_gpsimd=False):
            psg[tg, g] = t4.tile([P, W, 4], BF16, name="t4", align_bytes=64)
            dst, src = psg[tg, g][:], psraw[tg, g][:]
            if on_gpsimd:
                nc.gpsimd.tensor_scalar(
                    out=dst, in0=src.rearrange("p t n -> p n t"), scalar1=1.0, scalar2=0.0, op0=ALU.mult, op1=ALU.add
                )
            else:
                nc.vector.tensor_copy(
                    out=dst.rearrange("p (c i) t -> p c t i", i=4), in_=src.rearrange("p t (c i) -> p c t i", i=4)
                )

        def ps_quant(tg, g):
            quantize(psq[tg, g], 0, W, psg[tg, g][:].rearrange("p n t -> p (n t)"))

        graw, gacc, gg = {}, {}, {}

        def g_open(gi, k, jg):
            gacc[gi, k, jg] = ps.tile([P, W], F32, name="bank")

        def g_pass(gi, k, jg, c):
            mx(gacc[gi, k, jg][:], wdq[gi, c], k * P, wq[jg, c], 0, W, c == 0, c == NC - 1)

        def g_unit(gi, k, jg):
            g_open(gi, k, jg)
            for c in range(NC):
                g_pass(gi, k, jg, c)

        def g_out(gi, k, jg, on_vector=False):
            if (gi, jg) not in graw:
                graw[gi, jg] = t4.tile([P, 4, W], BF16, name="t4", align_bytes=64)
            dst, src = graw[gi, jg][:, k, :], gacc[gi, k, jg][:]
            col = t_cols[:, gi, k : k + 1]
            if on_vector:
                nc.vector.tensor_scalar(out=dst, in0=src, scalar1=col, scalar2=None, op0=ALU.mult)
            else:
                nc.scalar.activation(out=dst, in_=src, func=ACT.Copy, scale=col)

        def g_group(gi, jg):
            gg[gi, jg] = t4.tile([P, W, 4], BF16, name="t4", align_bytes=64)
            nc.vector.tensor_copy(
                out=gg[gi, jg][:].rearrange("p (c i) t -> p c t i", i=4),
                in_=graw[gi, jg][:].rearrange("p t (c i) -> p c t i", i=4),
            )

        def g_quant(gi, jg):
            quantize(gq[gi, jg], 0, W, gg[gi, jg][:].rearrange("p n t -> p (n t)"))

        hbank, hr, racc, outs = {}, {}, {}, {}
        out_v = out.rearrange("(a m t) (h f) -> a m t h f", a=2, t=4, h=2)

        def r_unit(tg, q, g):
            acc = ps.tile([P, 4, P], F32, name="bank")
            racc[tg, q, g] = acc
            for k in range(4):
                for gi in range(2):
                    mx(acc[:, k, :], gq[gi, g], k * P, psq[tg, gi], q * P, P, gi == 0, gi == 1)

        def r_sum(tg, q, g):
            h = h0t[tg, g][:, q, :, :]
            nc.vector.scalar_tensor_tensor(
                out=h, in0=racc[tg, q, g][:], scalar=-0.5, in1=h, op0=ALU.mult, op1=ALU.add
            )

        rcopy = {}

        def r_copy(tg, q, g):
            rcopy[tg, q, g] = hp.tile([P, 4, P], F32, name="rc")
            nc.scalar.activation(out=rcopy[tg, q, g][:], in_=racc[tg, q, g][:], func=ACT.Copy, scale=-0.5)

        def r_add(tg, q, g):
            h = h0t[tg, g][:, q, :, :]
            nc.gpsimd.tensor_tensor(out=h, in0=h, in1=rcopy[tg, q, g][:], op=ALU.add)

        def h_turn(tg, q, g):
            bank = ps.tile([P, 4, P], F32, name="bank")
            hbank[tg, q, g] = bank
            for k in range(4):
                nc.tensor.transpose(bank[:, k, :], h0t[tg, g][:, q, k, :], ident[:])

        def h_out(tg, q):
            hr[tg, q] = hp.tile([P, W], F32, name="hr")
            nc.scalar.copy(
                out=hr[tg, q][:].rearrange("p (m t) -> p m t", t=4),
                in_=hbank[tg, q, 1][:].rearrange("p t m -> p m t"),
            )

        def r_pick(tg, q, side):
            if (tg, side) not in outs:
                outs[tg, side] = t8.tile([P, 4, W], F32, name="t8", align_bytes=64)
            o = outs[tg, side]
            nc.vector.tensor_tensor(
                out=o[:, q, :].rearrange("p (m t) -> p m t", t=4),
                in0=hbank[tg, q, 0][:].rearrange("p t m -> p m t"),
                in1=hr[tg, q][:].rearrange("p (m t) -> p m t", t=4),
                op=ALU.min if side else ALU.max,
            )
            nc.sync.dma_start(out=out_v[tg, :, q, side, :], in_=o[:, q, :])

        words_v = [out_words[tg].rearrange("p m t -> p (m t)").bitcast(I32) for tg in range(2)]
        scales_v = [out_scales[tg].bitcast(I32) for tg in range(2)]
        ob = {}

        def o_group(tg, side, half, eng):
            if (tg, side) not in ob:
                ob[tg, side] = t4.tile([P, W, 4], BF16, name="t4", align_bytes=64)
            cols = slice(half * 256, half * 256 + 256)
            dst, src = ob[tg, side][:, cols, :], outs[tg, side][:, :, cols]
            if eng == "g":
                nc.gpsimd.tensor_scalar(
                    out=dst, in0=src.rearrange("p t f -> p f t"), scalar1=1.0, scalar2=0.0, op0=ALU.mult, op1=ALU.add
                )
            else:
                dst = dst.rearrange("p (c i) t -> p c t i", i=4)
                src = src.rearrange("p t (c i) -> p c t i", i=4)
                if eng == "v":
                    nc.vector.tensor_copy(out=dst, in_=src)
                else:
                    nc.scalar.copy(out=dst, in_=src)

        def o_quant(tg, side):
            oq = oqp.tile([P, W], U32, name="oq", align_bytes=64)
            osc = oqp.tile([P, W], U8, name="osc", align_bytes=64)
            quantize((oq, osc), 0, W, ob[tg, side][:].rearrange("p n t -> p (n t)"))
            nc.sync.dma_start(out=words_v[tg][:, side * W : side * W + W], in_=oq[:].bitcast(I32))
            for quad in range(4):
                nc.sync.dma_start(
                    out=scales_v[tg][4 * quad : 4 * quad + 4, side * P : side * P + P],
                    in_=osc[32 * quad : 32 * quad + 4, :].bitcast(I32),
                )

        with tc.manual_schedule():
            w_group(0, 0, False)
            w_group(0, 1, True)
            wd_make(0, 0)
            w_quant(0, 0)
            wd_quant(0, 0)
            x_turn(0, 0, 0)
            wd_make(0, 1)
            g_open(0, 2, 0)
            g_pass(0, 2, 0, 0)
            w_group(0, 2, True)
            w_quant(0, 1)
            g_open(0, 3, 0)
            g_pass(0, 3, 0, 0)
            wd_quant(0, 1)
            x_turn(0, 0, 1)
            x_out(0, 0, 0, True)
            x_turn(0, 1, 0)
            x_out(0, 0, 1, True)
            g_open(0, 0, 0)
            g_pass(0, 0, 0, 0)
            x_out(0, 1, 0, False)
            g_pass(0, 3, 0, 1)
            wd_make(0, 2)
            g_pass(0, 2, 0, 1)
            w_group(0, 3, True)
            g_pass(0, 0, 0, 1)
            x_turn(0, 1, 1)
            w_quant(0, 2)
            x_turn(0, 2, 0)
            wd_quant(0, 2)
            x_turn(0, 3, 1)
            x_quant(0, 0)
            g_open(0, 1, 0)
            g_pass(0, 1, 0, 0)
            g_pass(0, 1, 0, 1)
            x_out(0, 1, 1, False)
            wd_make(0, 3)
            x_turn(0, 3, 0)
            x_out(0, 3, 1, False)
            x_turn(0, 2, 1)
            x_out(0, 3, 0, False)
            x_quant(0, 1)
            g_pass(0, 1, 0, 2)
            x_out(0, 2, 1, False)
            g_pass(0, 2, 0, 2)
            x_out(0, 2, 0, True)
            p_open(0, 0)
            p_pass(accs[0, 0], 0, 0, 0)
            w_group(1, 1, True)
            p_open(0, 2)
            p_pass(accs[0, 2], 0, 2, 0)
            wd_quant(0, 3)
            p_open(0, 3)
            p_pass(accs[0, 3], 0, 3, 0)
            p_pass(accs[0, 3], 0, 3, 1)
            w_quant(0, 3)
            g_pass(0, 3, 0, 2)
            p_pass(accs[0, 2], 0, 2, 1)
            x_quant(0, 2)
            g_pass(0, 0, 0, 2)
            p_open(0, 1)
            p_pass(accs[0, 1], 0, 1, 0)
            x_quant(0, 3)
            g_pass(0, 0, 0, 3)
            p_pass(accs[0, 1], 0, 1, 1)
            w_group(1, 2, False)
            g_pass(0, 3, 0, 3)
            g_out(0, 0, 0, False)
            g_pass(0, 2, 0, 3)
            p_pass(accs[0, 0], 0, 0, 1)
            w_group(1, 3, True)
            p_pass(accs[0, 1], 0, 1, 2)
            g_pass(0, 1, 0, 3)
            w_quant(1, 1)
            p_pass(accs[0, 2], 0, 2, 2)
            p_pass(accs[0, 1], 0, 1, 3)
            g_out(0, 1, 0, True)
            p_pass(accs[0, 2], 0, 2, 3)
            p_pass(accs[0, 3], 0, 3, 2)
            w_group(1, 0, False)
            x_turn(1, 1, 0)
            x_turn(1, 0, 0)
            x_out(1, 1, 0, False)
            p_pass(accs[0, 0], 0, 0, 2)
            w_quant(1, 3)
            g_out(0, 2, 0, False)
            p_pass(accs[0, 0], 0, 0, 3)
            x_turn(1, 2, 0)
            w_quant(1, 0)
            g_out(0, 3, 0, False)
            w_quant(1, 2)
            x_turn(1, 2, 1)
            x_out(1, 2, 0, False)
            x_turn(1, 1, 1)
            wd_make(1, 2)
            p_scale(0, 0, False)
            p_pass(accs[0, 3], 0, 3, 3)
            g_unit(0, 3, 1)
            x_out(1, 1, 1, False)
            x_out(1, 0, 0, False)
            x_quant(1, 1)
            g_unit(0, 0, 1)
            p_scale(0, 3, False)
            wd_make(1, 3)
            p_scale(0, 1, False)
            g_unit(0, 1, 1)
            x_out(1, 2, 1, False)
            wd_quant(1, 2)
            p_keep(0, 3, False)
            wd_quant(1, 3)
            p_unit(0, 6)
            g_out(0, 3, 1, False)
            p_keep(0, 1, True)
            g_out(0, 0, 1, False)
            wd_make(1, 0)
            g_unit(0, 2, 1)
            p_scale(0, 6, False)
            wd_make(1, 1)
            x_turn(1, 0, 1)
            g_out(0, 2, 1, False)
            x_turn(1, 3, 0)
            x_quant(1, 2)
            x_turn(1, 3, 1)
            wd_quant(1, 0)
            p_unit(0, 7)
            x_out(1, 3, 1, False)
            wd_quant(1, 1)
            p_scale(0, 2, False)
            x_out(1, 3, 0, True)
            p_unit(0, 5)
            x_out(1, 0, 1, False)
            g_group(0, 0)
            g_out(0, 1, 1, False)
            g_unit(1, 0, 1)
            p_scale(0, 5, False)
            g_group(0, 1)
            p_keep(0, 0, False)
            g_unit(1, 1, 1)
            g_out(1, 0, 1, False)
            p_scale(0, 7, True)
            g_unit(1, 3, 0)
            x_quant(1, 3)
            p_keep(0, 7, False)
            g_out(1, 1, 1, True)
            p_unit(0, 4)
            x_quant(1, 0)
            ps_group(0, 0, False)
            g_unit(1, 3, 1)
            p_keep(0, 6, True)
            g_unit(1, 2, 1)
            g_out(1, 3, 1, False)
            g_quant(0, 0)
            ps_quant(0, 0)
            p_unit(1, 3)
            g_out(1, 2, 1, False)
            p_keep(0, 5, False)
            p_unit(1, 2)
            g_group(1, 1)
            p_keep(0, 2, False)
            p_scale(0, 4, False)
            g_unit(1, 1, 0)
            ps_group(0, 1, False)
            p_unit(1, 1)
            g_out(1, 1, 0, False)
            p_scale(1, 3, True)
            p_scale(1, 2, False)
            p_unit(1, 0)
            p_scale(1, 1, True)
            g_quant(0, 1)
            p_unit(1, 4)
            p_scale(1, 0, False)
            p_keep(1, 1, True)
            p_keep(0, 4, False)
            ps_quant(0, 1)
            g_unit(1, 2, 0)
            p_scale(1, 4, False)
            g_quant(1, 1)
            ps_group(1, 0, False)
            p_unit(1, 7)
            g_out(1, 2, 0, False)
            p_keep(1, 2, False)
            g_unit(1, 0, 0)
            g_out(1, 3, 0, True)
            p_keep(1, 0, False)
            ps_quant(1, 0)
            p_unit(1, 5)
            g_out(1, 0, 0, False)
            p_scale(1, 7, False)
            p_unit(1, 6)
            g_group(1, 0)
            p_scale(1, 5, False)
            r_unit(0, 3, 1)
            p_keep(1, 5, False)
            r_unit(0, 0, 1)
            g_quant(1, 0)
            p_scale(1, 6, False)
            r_unit(0, 2, 1)
            r_copy(0, 3, 1)
            ps_group(1, 1, False)
            p_keep(1, 6, False)
            r_unit(0, 1, 0)
            r_add(0, 3, 1)
            r_copy(0, 2, 1)
            r_unit(0, 1, 1)
            r_copy(0, 0, 1)
            r_unit(0, 2, 0)
            ps_quant(1, 1)
            r_add(0, 2, 1)
            r_copy(0, 1, 1)
            r_unit(0, 3, 0)
            p_keep(1, 4, True)
            p_keep(1, 7, False)
            r_sum(0, 1, 0)
            r_unit(0, 0, 0)
            r_add(0, 1, 1)
            r_sum(0, 2, 0)
            r_unit(1, 1, 1)
            r_sum(0, 3, 0)
            r_unit(1, 3, 1)
            r_add(0, 0, 1)
            h_turn(0, 2, 1)
            r_sum(1, 3, 1)
            h_turn(0, 1, 0)
            h_turn(0, 1, 1)
            h_out(0, 2)
            r_sum(0, 0, 0)
            h_turn(0, 2, 0)
            h_turn(0, 3, 1)
            h_out(0, 1)
            r_unit(1, 0, 1)
            r_pick(0, 2, 0)
            p_keep(1, 3, False)
            r_pick(0, 1, 0)
            r_unit(1, 0, 0)
            r_copy(1, 1, 1)
            r_pick(0, 2, 1)
            r_unit(1, 1, 0)
            r_copy(1, 0, 1)
            r_add(1, 1, 1)
            r_sum(1, 0, 0)
            h_out(0, 3)
            h_turn(0, 0, 1)
            r_sum(1, 1, 0)
            h_turn(0, 0, 0)
            r_unit(1, 2, 1)
            h_out(0, 0)
            r_add(1, 0, 1)
            r_pick(0, 1, 1)
            h_turn(0, 3, 0)
            r_pick(0, 0, 0)
            r_copy(1, 2, 1)
            h_turn(1, 1, 1)
            r_unit(1, 2, 0)
            r_pick(0, 3, 0)
            r_add(1, 2, 1)
            r_pick(0, 0, 1)
            r_unit(1, 3, 0)
            o_group(0, 0, 0, "s")
            r_pick(0, 3, 1)
            h_turn(1, 0, 1)
            o_group(0, 0, 1, "g")
            r_sum(1, 2, 0)
            h_turn(1, 3, 1)
            h_out(1, 1)
            h_turn(1, 1, 0)
            r_sum(1, 3, 0)
            h_turn(1, 2, 1)
            h_out(1, 0)
            h_turn(1, 0, 0)
            r_pick(1, 1, 0)
            o_group(0, 1, 0, "g")
            h_turn(1, 2, 0)
            h_out(1, 2)
            o_quant(0, 0)
            h_turn(1, 3, 0)
            h_out(1, 3)
            r_pick(1, 2, 0)
            o_group(0, 1, 1, "s")
            r_pick(1, 0, 0)
            r_pick(1, 3, 0)
            r_pick(1, 1, 1)
            o_group(1, 0, 0, "s")
            r_pick(1, 3, 1)
            o_quant(0, 1)
            o_group(1, 0, 1, "s")
            r_pick(1, 2, 1)
            r_pick(1, 0, 1)
            o_quant(1, 0)
            o_group(1, 1, 1, "v")
            o_group(1, 1, 0, "v")
            o_quant(1, 1)
